import numpy as np, ml_dtypes
CORES = [35,38,43,46]
N = 4
BF = ml_dtypes.bfloat16
def gentries(a):
    return np.ascontiguousarray(a.reshape(8, 16, -1).transpose(0, 2, 1)).reshape(8, -1)
def gtable(e):
    e = np.asarray(e); return np.ascontiguousarray(e.reshape(8, -1, 16).transpose(0, 2, 1)).reshape(128, -1).astype(np.int32)
W, K, RO, S, TH, AG = 3072, 256, 3, 4, 68, 9
L0 = 16 - RO
B = K // N
def hubbed(rng, hub, n, share):
    return np.where(rng.random((N, 8, n)) < share, np.take_along_axis(hub, rng.integers(0, 32, (N, 8, n)), 2), rng.integers(0, W, (N, 8, n)))
def parts(rng):
    x = np.where(rng.random((N, 8, 1, W)) < 0.875, rng.integers(0, 16, (N, 8, 16, W)), rng.integers(4, 12, (N, 8, 16, W)))
    hub = rng.integers(0, W, (N, 8, 32)); a = hubbed(rng, hub, L0 * W, 0.1).reshape(N, 8, L0, W)
    a = np.where(rng.random(a.shape) < rng.choice(np.array([0.05, 0.2, 0.45]), (N, 8, 1, 1)), -1, a)
    return x, a, hubbed(rng, hub, W, 0.25), rng.integers(0, W, (N, 8, K))
def pack(x, a, s, p):
    a = np.concatenate([a, np.full((N, 8, RO, W), -1)], axis=2)
    return {"x0": np.ascontiguousarray(x.reshape(N, 128, W)).astype(np.float32).astype(BF), "lk": np.ascontiguousarray(a.reshape(N, 128, W)).astype(np.int32),
            "nx": np.ascontiguousarray(s).astype(np.int32), "w0": np.stack([gtable(e) for e in p])}
def setup_inputs(rng):
    return pack(*parts(rng))
def setup_inputs_ties(rng):
    x, a, s, p = parts(rng); h = W // 2
    x[..., :h] = rng.integers(0, 16, (N, 8, 16, h))
    t = TH - 1 + rng.integers(0, 3, (N, 8, 1, h)); o = np.argsort(rng.random((N, 8, 16, h)), axis=2)
    x[..., h:2 * h] = x[..., :h] + np.where(x[..., :h] < 8, 1, -1) * ((t >> 4) + (o < (t & 15)))
    i = np.arange(L0)[None, None, :, None]; at = rng.integers(0, L0, (N, 8, 1, h)); bare = rng.random((N, 8, 1, h)) < 0.5
    a[..., :h] = np.where(i == at, h + np.arange(h), np.where((i > at) | bare, -1, a[..., :h]))
    return pack(x, a, s, rng.integers(0, h, (N, 8, K)))
def setup_inputs_votes(rng):
    x, a, s, p = parts(rng); h = K // 2
    for q in range(N):
        for g in range(8):
            if q < N - 1 and g % 4 == 3: continue
            c = rng.permutation(W)[:K * (S + 1)].reshape(K, S + 1); a[q, g] = -1
            s[q, g, c[:, :S]] = c[:, 1:]
            if q == N - 1:
                y = rng.integers(5, 8, (16, K, S)); e = np.where(np.arange(K) < h, 15, rng.integers(8, 11, (16, K)))
                s[q, g, c[:h, S]] = c[h + rng.permutation(h), 2]
                p[q, g] = c[:, 0]
            elif g % 2 == 1:
                n = K - 1 if g == 1 else int(rng.integers(h, K))
                y = rng.integers(0, 8, (16, K, S)); y[rng.permutation(16)[AG - 1:], n] += 8
                e = rng.integers(0, 16, (16, K)); e[:, 0] = 8
                s[q, g, c[:, S - 1]] = c[0, S]
                p[q, g] = c[:, 0]
            else:
                y = rng.integers(2, 14, (16, K, S)); y[:, h:] = np.where(rng.random((1, K - h, 1)) < 0.5, 2, 13)
                z = y[:, :, 0]
                for k in range(1, S): z = (z + y[:, :, k]) >> 1
                o = np.argsort(rng.random((16, K)), axis=0); n = AG - 1 + rng.integers(0, 3, (1, K))
                e = z + np.where(o < n, rng.integers(1, 3, (16, K)), -rng.integers(0, 2, (16, K)))
                s[q, g, c[h:, S - 1]] = np.where(rng.random(K - h) < 0.75, c[:K - h, S], c[h:, S])
                p[q, g] = c[rng.permutation(K), 0]
            x[q, g][:, c[:, :S].reshape(-1)] = y.reshape(16, K * S); x[q, g][:, c[:, S]] = e
    return pack(x, a, s, p)
def setup_inputs_alike(rng):
    x, a, s, p = parts(rng); few = np.array([0, W - 1, W // 2, 5])
    a[:, ::2] = np.where(a[:, ::2] < 0, -1, rng.choice(few, (N, 4, L0, W)))
    a[:, 1] = np.where(a[:, 1] < 0, -1, np.arange(W)); s[:, 1] = np.arange(W)
    s[:, 0] = W - 1; s[:, 4] = 0; s[:, 2] = rng.choice(few, (N, W))
    p[:, 3] = p[:, 3, :1]; p[:, 5] = rng.choice(few, (N, K)); p[:, 6] = np.where(rng.random((N, K)) < 0.5, 0, W - 1)
    return pack(x, a, s, p)
def setup_inputs_full(rng):
    x, a, s, p = parts(rng)
    x[:, ::2] = rng.integers(6, 10, (N, 4, 16, W)); x[:, 1::2] = 15 * rng.integers(0, 2, (N, 4, 16, W))
    a = np.where(a < 0, rng.integers(0, W, a.shape), a)
    return pack(x, a, s, p)
def setup_inputs_spread(rng):
    x, a, s, p = parts(rng)
    x = np.minimum((np.exp2(1 + 3 * rng.random((N, 8, 1, W))) * rng.random((N, 8, 16, W))).astype(np.int64), 15)
    a = np.where(a < 0, -1, (W * rng.random(a.shape) ** 3).astype(np.int64)); s = (W * rng.random(s.shape) ** 2).astype(np.int64)
    return pack(x, np.minimum(a, W - 1), np.minimum(s, W - 1), p)
def check_inputs(d):
    bad = []
    x = d["x0"].astype(np.float32)
    if not np.all((x >= 0) & (x <= 15) & (x == np.floor(x))): bad.append("x0 whole numbers from 0 to 15")
    for k, lo in (("lk", -1), ("nx", 0), ("w0", 0)):
        if np.min(d[k]) < lo or np.max(d[k]) > W - 1: bad.append("range of " + k)
    if np.any(d["lk"].reshape(-1, 8, 16, W)[:, :, L0:] != -1): bad.append("upper links of lk empty")
    return bad
def reference(x0, lk, nx, w0):
    M = W + RO * K
    X = np.zeros((N, 8, 16, M), np.int64); X[..., :W] = x0.astype(np.float32).astype(np.int64).reshape(N, 8, 16, W)
    ad = np.full((N, 8, 16, M), -1, np.int64); ad[..., :W] = lk.reshape(N, 8, 16, W)
    sc = np.zeros((N, 8, M), np.int64); sc[..., :W] = nx
    v = np.stack([gentries(e) for e in w0]).astype(np.int64)
    i = np.arange(16)[:, None]
    for t in range(RO):
        n = W + t * K; Z = np.zeros((N, 8, 16, K), np.int64)
        for r in range(N):
            for g in range(8):
                x, a, s, p = X[r, g], ad[r, g], sc[r, g], v[r, g]
                z = x[:, p]; l = np.full(K, 16)
                for k in range(S):
                    c = a[:, p]
                    dist = np.add.reduce(np.abs(x[:, np.maximum(c, 0)] - z[:, None, :]), axis=0)
                    b = np.max(np.where((c >= 0) & (dist < TH) & (i < l), i, -1), axis=0)
                    p = np.where(b >= 0, c[np.maximum(b, 0), np.arange(K)], s[p]); l = np.where(b >= 0, b, l)
                    y = x[:, p]; yes = np.add.reduce((y > z).astype(np.int64), axis=0) >= AG
                    z = (z + y) >> 1
                Z[r, g] = z; v[r, g] = p
                ends = np.zeros(M, bool); ends[p] = True
                no = np.zeros(M, bool); no[p[~yes]] = True
                x[::2] = np.where(ends & ~no, 15 - x[::2], x[::2])
                u, first = np.unique(p, return_index=True)
                a[L0 + t, u] = n + first; s[n:n + K] = s[p]
        for r in range(N):
            for q in range(N):
                X[q, :, :, n + r * B:n + (r + 1) * B] = np.roll(Z[r, :, :, q * B:(q + 1) * B], (q - r) % N, axis=0)
    return {"yx": X.reshape(N, 128, M).astype(np.float32).astype(BF), "yv": v.astype(np.float32)}

@@ -1,0 +1,560 @@
+import numpy as np
+from concourse.bass import DstId, RemoteDMATransfer
+from concourse.mybir import AluOpType, ActivationFunctionType
+
+ALU = AluOpType
+ACT = ActivationFunctionType
+
+W0N, K, RO, S = 3072, 256, 3, 4
+NU = 4
+W = K // NU
+WB = W // 16
+B = 272
+CEN = 1919
+NM = 15
+GC = 7
+MC = 256 // W
+XC = B + W0N + RO * K
+AC = B + W0N + (RO - 1) * K
+CYC = 0.00083
+PEC = 0.00045
+GAT = 1.4
+WK = 0.2
+LOOK = 0.02
+
+SCRATCH = {}
+
+
+def _b(name, cols, dtype, where="sbuf"):
+    SCRATCH[name] = (where, [128, cols], dtype)
+
+
+_b("X", XC, "bfloat16")
+_b("A", AC, "int32")
+_b("WL", 16, "int32")
+for _n in ("NL", "OFF", "OFX"):
+    _b(_n, 16, "uint16")
+for _n in ("z", "ok", "s", "gt", "yg", "sel0", "sel1", "sel2", "sel3", "VX"):
+    _b(_n, 256, "bfloat16")
+for _n in ("AT", "T1", "sA", "vb", "MKl", "MK2"):
+    _b(_n, 256, "float16")
+_b("LT", 256, "uint16")
+_b("xg", 15 * 256, "bfloat16")
+_b("mn", 15 * 256, "bfloat16")
+for _u in range(NU):
+    _b("pd%d" % _u, 512, "float32", "psum")
+    _b("pc%d" % _u, 512, "float32", "psum")
+for _n in ("vT", "vX", "wt", "ofs", "fd", "fe", "ff", "fm", "fo", "TR"):
+    _b(_n, 16, "float32")
+_b("EQ", 16 * 256, "bfloat16")
+for _n in ("sc", "sv", "s2", "scL", "scM", "AF", "VA", "vout", "J", "JM", "ta", "tb", "tc", "td", "RS", "NW0", "NW1"):
+    _b(_n, 256, "float32")
+_b("snd", 192, "bfloat16")
+_b("PI", 4, "int32")
+_b("col", 32, "float32")
+_b("JG", 128, "float32")
+_b("JP", 128, "float32")
+_b("W1", 144, "bfloat16")
+_b("W2", 144, "bfloat16")
+for _n in ("BOb", "NBb", "FBb", "MTb", "ZS", "DEAD", "TRI0", "TRI1", "TRI2", "IDb", "PM1", "PM2", "PM3"):
+    _b(_n, 128, "bfloat16")
+for _n in ("BOh", "IDh", "SW00", "SW01", "SW10", "SW11", "MK0"):
+    _b(_n, 128, "float16")
+
+SEMAPHORES = ["qV", "qS", "qP", "qG", "dX", "dW", "dA", "dO", "arr0", "arr1", "arr2", "snt"]
+
+
+def rank_program(g, core, T, topo):
+    rank = T.rank_of(core)
+    if rank is None:
+        return
+    QUE = {"V": g.vector, "S": g.scalar, "P": g.tensor, "G": g, "Y": g.sync}
+    recs = []
+    stage = [0]
+
+    def rec(q, kind, fn, reads, writes, dur, lat=0.0, sem=None):
+        recs.append((q, kind, fn, tuple(reads), tuple(writes), dur, lat, sem, stage[0]))
+
+    def op(q, fn, reads, writes, dur):
+        rec(q, "op", fn, reads, writes, dur)
+
+    def dma(q, out, in_, sem, reads, writes, lat):
+        rec(q, "dma", lambda: QUE[q].dma_start(out, in_), reads, writes, 0.06, lat, sem)
+
+    def vd(n, f=1.0, ind=None):
+        return max(64, n * f) * CYC if ind is None else 0.05 + n * CYC * ind
+
+    def ts(out, in0, s1, s2, op0, op1, reads, writes, n=128, f=1.0, ind=None):
+        if op1 is None:
+            op("V", lambda: g.vector.tensor_scalar(out, in0, s1, s2, op0), reads, writes, vd(n, f, ind))
+        else:
+            op("V", lambda: g.vector.tensor_scalar(out, in0, s1, s2, op0, op1), reads, writes, vd(n, f, ind))
+
+    def tt(out, in0, in1, o, reads, writes, n=128, f=1.0, ind=None):
+        op("V", lambda: g.vector.tensor_tensor(out, in0, in1, o), reads, writes, vd(n, f, ind))
+
+    def cp(out, in_, reads, writes, n, ind=None):
+        op("V", lambda: g.vector.tensor_copy(out, in_), reads, writes, vd(n, 1.0, ind))
+
+    def act(out, in_, f, bias, scale, reads, writes, n=128, ind=1.0):
+        op("S", lambda: g.scalar.activation(out, in_, f, bias=bias, scale=scale), reads, writes, 0.065 + n * CYC * ind)
+
+    def scn(out, data1, n, reads, writes):
+        op("V", lambda: g.vector.tensor_tensor_scan(out, T.RS[:, 0:n], data1, 0.0, ALU.mult, ALU.max), ["RS"] + reads, writes, vd(n))
+
+    def mms(lst, reads, writes, n=128):
+        def go():
+            r = None
+            for (o, l, r_, st, sp) in lst:
+                r = g.tensor.matmul(o, l, r_, st, sp)
+            return r
+        op("P", go, reads, writes, len(lst) * max(n, 64) * PEC)
+
+    dma("Y", T.WL[:], T.w0[:], "dW", [], ["WL"], 2.0)
+    dma("Y", T.X[:, B:B + W0N], T.x0[:], "dX", [], ["X"], 5.0)
+    for gr in range(8):
+        dma("S" if gr % 2 == 0 else "Y", T.A[16 * gr:16 * gr + 15, B:B + W0N], T.lk[16 * gr:16 * gr + 15, :], "dA", [], ["A%d" % gr], 9.0)
+    dma("S", T.A[15:128:16, B:B + W0N], T.nx[:], "dA", [], ["A8"], 9.0)
+    AK = ["A%d" % i for i in range(9)] + ["Am"]
+    XK = ["X", "Xm"]
+
+    CI = {}
+
+    def newcol(name):
+        CI[name] = len(CI)
+        return col(name)
+
+    def col(name):
+        i = CI[name]
+        return T.col[:, i:i + 1]
+
+    def iota(ap, key, pattern, base, cm, n, whole=False):
+        if whole:
+            op("G", lambda: g.iota(ap, pattern, base, cm), [], [key], 0.13 + 2 * CYC * n)
+        else:
+            op("G", lambda: g.iota(ap, pattern, base, cm, allow_small_or_imprecise_dtypes=True), [], [key], 0.13 + 2 * CYC * n)
+
+    iota(T.PI[:, 0:1], "PI", [[0, 1]], 0, 1, 1, True)
+    iota(T.JG[:], "JG", [[16, 8], [0, 16]], 0, 0, 128)
+    iota(T.J[:], "J", [[1, 256]], 0, 0, 256)
+    iota(T.JM[:], "JM", [[0, 16], [1, 16]], 0, 0, 256)
+
+    def mkcol(name, in0, s1, s2, op0, op1, reads):
+        ts(newcol(name), in0, s1, s2, op0, op1, reads, ["c" + name], 1)
+
+    ts(T.NL[:], T.WL[:], float(B), None, ALU.add, None, ["WL"], ["NL%d" % u for u in range(NU)], 16)
+    op("V", lambda: g.vector.memset(T.A[:, 0:B], -1), [], ["Am"], vd(B))
+    op("V", lambda: g.vector.memset(T.X[:, 0:B], 95.0), [], ["Xm"], vd(B, 0.5))
+    ts(T.PI[:, 1:2], T.PI[:, 0:1], 15, None, ALU.bitwise_and, None, ["PI"], ["PI1"], 1)
+    ts(T.PI[:, 2:3], T.PI[:, 0:1], 16, None, ALU.bitwise_and, None, ["PI"], ["PI2"], 1)
+    ts(T.PI[:, 3:4], T.PI[:, 0:1], 1, None, ALU.bitwise_and, None, ["PI"], ["PI3"], 1)
+    for n_, a in (("P", 0), ("Pm16", -16), ("Pp16", 16), ("Pp32", 32), ("Pp48", 48), ("Pm112", -112), ("Pm96", -96), ("Pm80", -80)):
+        mkcol(n_, T.PI[:, 0:1], float(a), None, ALU.add, None, ["PI"])
+    mkcol("R", T.PI[:, 1:2], 0.0, None, ALU.add, None, ["PI1"])
+    mkcol("U1", T.PI[:, 2:3], 0.0625, None, ALU.mult, None, ["PI2"])
+    mkcol("U0", T.PI[:, 2:3], -0.0625, 1.0, ALU.mult, ALU.add, ["PI2"])
+    mkcol("fs", T.PI[:, 3:4], 2.0, -1.0, ALU.mult, ALU.add, ["PI3"])
+    mkcol("fb", T.PI[:, 3:4], -335.0, 175.0, ALU.mult, ALU.add, ["PI3"])
+    tt(newcol("G"), col("P"), col("R"), ALU.subtract, ["cP", "cR"], ["cG"], 1)
+    mkcol("G15", col("G"), 15.0, None, ALU.add, None, ["cG"])
+    mkcol("m15", col("R"), 15.0, None, ALU.is_equal, None, ["cR"])
+    mkcol("m15m", col("m15"), -1.0, None, ALU.add, None, ["cm15"])
+    for t in range(RO - 1):
+        mkcol("r%d" % t, col("R"), float(13 + t), None, ALU.is_equal, None, ["cR"])
+        mkcol("nr%d" % t, col("R"), float(13 + t), None, ALU.not_equal, None, ["cR"])
+    mkcol("d128", col("R"), 15.0, 128.0, ALU.is_lt, ALU.mult, ["cR"])
+    mkcol("x16", col("m15"), -16.0, None, ALU.mult, None, ["cm15"])
+    tt(newcol("RP"), col("R"), col("x16"), ALU.add, ["cR", "cx16"], ["cRP"], 1)
+    J1, JM1 = T.J[:, 0:128], T.JM[:, 0:128]
+    for u, h, n_ in ((0, 0, "P"), (1, 1, "P"), (0, 1, "Pp16"), (1, 0, "Pm16")):
+        nm = "SW%d%d" % (u, h)
+        ts(T[nm][:], J1, col(n_), col("U%d" % u), ALU.is_equal, ALU.mult, ["J", "c" + n_, "cU%d" % u], [nm])
+    ts(T.IDb[:], J1, col("P"), None, ALU.is_equal, None, ["J", "cP"], ["IDb"])
+    ts(T.BOb[:], T.JG[:], col("G"), None, ALU.is_equal, None, ["JG", "cG"], ["BOb"])
+    ts(T.ta[:, 0:128], JM1, float(NM), None, ALU.is_lt, None, ["JM"], ["ta0"])
+    tt(T.ZS[:], T.ta[:, 0:128], T.BOb[:], ALU.mult, ["ta0", "BOb"], ["ZS"], 128, 2)
+    ts(T.W1[:], T.J[:, 0:144], col("G15"), None, ALU.is_equal, None, ["J", "cG15"], ["W1"], 144)
+    ts(T.W2[:], T.J[:, 0:144], col("G15"), -2.0, ALU.is_equal, ALU.mult, ["J", "cG15"], ["W2"], 144)
+    ts(T.tb[:, 0:128], JM1, 15.0, -16.0, ALU.is_equal, ALU.mult, ["JM"], ["tb0"])
+    tt(T.JP[:], T.tb[:, 0:128], JM1, ALU.add, ["tb0", "JM"], ["JP"], 128, 2)
+    ts(T.ta[:, 128:256], T.JP[:], col("RP"), -2.0, ALU.is_lt, ALU.mult, ["JP", "cRP"], ["ta1"])
+    ts(T.tb[:, 128:256], T.JP[:], col("RP"), None, ALU.is_equal, None, ["JP", "cRP"], ["tb1"])
+    tt(T.tc[:, 0:128], T.ta[:, 128:256], T.tb[:, 128:256], ALU.add, ["ta1", "tb1"], ["tc0"], 128, 2)
+    tt(T.tc[:, 128:256], T.tc[:, 0:128], T.BOb[:], ALU.mult, ["tc0", "BOb"], ["tc1"], 128, 2)
+    for t in range(RO):
+        nm = "rv%d" % t
+        mkcol(nm, col("RP"), float(13 + t), None, ALU.is_lt, None, ["cRP"])
+        ts(T.td[:, 0:128], T.JP[:], float(13 + t), col(nm), ALU.is_lt, ALU.mult, ["JP", "c" + nm], ["td0"])
+        tt(T["TRI%d" % t][:], T.td[:, 0:128], T.tc[:, 128:256], ALU.mult, ["td0", "tc1"], ["TRI%d" % t], 128, 2)
+    ts(T.BOh[:], T.JG[:], col("G"), None, ALU.is_equal, None, ["JG", "cG"], ["BOh"])
+    ts(T.IDh[:], J1, col("P"), None, ALU.is_equal, None, ["J", "cP"], ["IDh"])
+    ts(T.ta[:], T.JM[:], col("R"), 8192.0 + CEN + 1, ALU.is_equal, ALU.mult, ["JM", "cR"], ["ta0", "ta1"], 256)
+    ts(T.MKl[:], T.ta[:], -8192.0, None, ALU.add, None, ["ta0", "ta1"], ["MKl"], 256)
+    ts(T.RS[:], T.JM[:], 0.0, None, ALU.is_gt, None, ["JM"], ["RS"], 256)
+    ts(T.tb[:, 0:128], JM1, col("R"), col("d128"), ALU.is_ge, ALU.mult, ["JM", "cR", "cd128"], ["tb0"])
+    ts(T.tb[:, 128:256], JM1, 15.0, None, ALU.is_lt, None, ["JM"], ["tb1"])
+    tt(T.tc[:, 0:128], T.tb[:, 0:128], T.tb[:, 128:256], ALU.mult, ["tb0", "tb1"], ["tc0"], 128, 2)
+    tt(T.DEAD[:], T.tc[:, 0:128], T.BOb[:], ALU.mult, ["tc0", "BOb"], ["DEAD"], 128, 2)
+    stage[0] = 5
+    ts(T.tb[:, 128:256], JM1, col("R"), 8192.0, ALU.is_equal, ALU.mult, ["JM", "cR"], ["tb1"])
+    ts(T.MK0[:], T.tb[:, 128:256], -8192.0, None, ALU.add, None, ["tb1"], ["MK0"])
+    ts(T.MK2[:], T.JM[:], col("R"), float(B - 1), ALU.is_equal, ALU.mult, ["JM", "cR"], ["MK2"], 256)
+    ts(T.NBb[:], T.JG[:], col("G"), -float(2 ** 23), ALU.is_equal, ALU.mult, ["JG", "cG"], ["NBb"])
+    ts(T.FBb[:], T.JG[:], col("G"), 2.0 ** -10, ALU.is_equal, ALU.mult, ["JG", "cG"], ["FBb"])
+    ts(T.ta[:, 0:128], JM1, col("R"), -float(2 ** 23), ALU.is_gt, ALU.mult, ["JM", "cR"], ["ta0"])
+    ts(T.ta[:, 128:256], JM1, col("R"), 2.0 ** -10, ALU.is_le, ALU.mult, ["JM", "cR"], ["ta1"])
+    tt(T.td[:, 128:256], T.ta[:, 0:128], T.ta[:, 128:256], ALU.add, ["ta0", "ta1"], ["td1"], 128, 2)
+    tt(T.MTb[:], T.td[:, 128:256], T.BOb[:], ALU.mult, ["td1", "BOb"], ["MTb"], 128, 2)
+    for d, n1, n2 in (("1", "Pp16", "Pm112"), ("2", "Pp32", "Pm96"), ("3", "Pp48", "Pm80")):
+        ts(T.ta[:, 0:128], J1, col(n1), None, ALU.is_equal, None, ["J", "c" + n1], ["ta0"])
+        ts(T.tb[:, 0:128], J1, col(n2), None, ALU.is_equal, None, ["J", "c" + n2], ["tb0"])
+        tt(T["PM" + d][:], T.ta[:, 0:128], T.tb[:, 0:128], ALU.add, ["ta0", "tb0"], ["PM" + d], 128, 2)
+    for t in range(RO - 1):
+        ts(T["NW%d" % t][:], T.J[:], float(W0N + K * t), col("r%d" % t), ALU.add, ALU.mult, ["J", "cr%d" % t], ["NW%d" % t], 256)
+    ts(T.tb[:, 128:144], T.J[:, 0:16], 16.0, None, ALU.mult, None, ["J"], ["tb1"], 16)
+    ts(T.TR[:], T.tb[:, 128:144], col("R"), None, ALU.add, None, ["tb1", "cR"], ["TR"], 16)
+
+    def un(name, u):
+        return T[name][:, W * u:W * u + W]
+
+    def tab(name, u):
+        return T[name][:, WB * u:WB * u + WB]
+
+    def last16(name, u):
+        return T[name][:, W * u + 15:W * u + W:16]
+
+    def pz(u, n):
+        return T["pc%d" % u][:, 0:n]
+
+    def pe(u):
+        return T["pc%d" % u][:, 256:256 + W]
+
+    def pc(u):
+        return T["pc%d" % u][:, 384:384 + W]
+
+    def xw(t):
+        return T.X[:, 0:B + W0N + K * t]
+
+    def aw(t):
+        return T.A[:, 0:B + W0N + K * t]
+
+    def prep(t, u):
+        s = str(u)
+        ts(un("AT", u), aw(t).indirect(tab("NL", u)), float(-CEN), None, ALU.add, None, AK + ["NL" + s], ["AT" + s], W, 1, GAT)
+        nb = W // 32
+        o = W * u
+        for b in range(nb):
+            op("V", lambda b=b: g.vector.transpose(T.T1[:, o + b:o + W:nb] if nb > 1 else T.T1[:, o:o + W],
+                                                   T.AT[:, o + 32 * b:o + 32 * b + 32]), ["AT" + s], ["T1%s%d" % (s, b)], vd(32))
+        lst = []
+        for v in range(2):
+            for h in range(2):
+                lst.append((T["pc" + s][:, 384 + v:384 + W:2], T["SW%d%d" % (v, h)][:],
+                            T.T1[:, o + W // 2 * h:o + W // 2 * h + W // 2], h == 0, h == 1))
+        mms(lst, ["T1%s%d" % (s, b) for b in range(nb)] + ["SW00", "SW01", "SW10", "SW11"], ["pc" + s], W // 2)
+        n = WB * (13 + t)
+        ts(T.LT[:, o:o + n], T["pc" + s][:, 384:384 + n], float(CEN + B), None, ALU.add, None, ["pc" + s], ["LT" + s], n)
+
+    def bulk(t, u, step):
+        s = str(u)
+        nl = 13 + t
+        o = 15 * W * u
+        pd = T["pd" + s][:, 0:W]
+        mms([(T["pc" + s][:, W * j:W * j + W], T.IDb[:], un("z", u), True, True) for j in range(MC)], ["IDb", "z" + s], ["pc" + s], W)
+        mms([(pd, T.ZS[:], un("z", u), True, False)], ["ZS", "z" + s], ["pd" + s], W)
+        for k in range(step):
+            mms([(pd, T.DEAD[:], un("sel%d" % k, u), False, False)], ["DEAD", "sel%d%s" % (k, s)], ["pd" + s], W)
+        n2 = min(NM, nl)
+        for a in range(0, n2, GC):
+            b = min(a + GC, n2)
+            x = "xg%s%d" % (s, a)
+            act(T.xg[:, o + W * a:o + W * b], xw(t).indirect(T.LT[:, W * u + WB * a:W * u + WB * b]), ACT.Identity, 160.0, 1.0,
+                XK + ["LT" + s], [x], W * (b - a), GAT)
+            for c in range(a, b, MC):
+                d = min(c + MC, b)
+                h = slice(o + W * c, o + W * d)
+                m = "mn%s%d" % (s, c)
+                tt(T.mn[:, h], T.xg[:, h], pz(u, W * (d - c)), ALU.min, [x, "pc" + s], [m], W * (d - c))
+                mms([(pd, T.W1[:, 15 - i:143 - i], T.xg[:, o + W * i:o + W * i + W], False, False) for i in range(c, d)],
+                    ["W1", x], ["pd" + s], W)
+                mms([(pd, T.W2[:, 15 - i:143 - i], T.mn[:, o + W * i:o + W * i + W], False, i == nl - 1) for i in range(c, d)],
+                    ["W2", m], ["pd" + s], W)
+        for i in range(n2, nl):
+            h = slice(o + W * i, o + W * i + W)
+            x, m = "xg%s%d" % (s, i), "mn%s%d" % (s, i)
+            tt(T.xg[:, h], xw(t).indirect(T.LT[:, W * u + WB * i:W * u + WB * i + WB]), un("z", u), ALU.subtract,
+               XK + ["LT" + s, "z" + s], [x], W, 1, GAT)
+            act(T.mn[:, h], T.xg[:, h], ACT.Abs, 160.0, 1.0, [x], [m], W)
+            mms([(pd, T.W1[:, 15 - i:143 - i], T.mn[:, h], False, i == nl - 1)], ["W1", m], ["pd" + s], W)
+
+    def choose(t, u, step):
+        s = str(u)
+        k = "sel%d" % step
+        ts(un("ok", u), T["pd" + s][:, 0:W], 68.0, None, ALU.is_lt, None, ["pd" + s], ["ok" + s], W)
+        mms([(pe(u), T["TRI%d" % t][:], un("ok", u), True, True)], ["TRI%d" % t, "ok" + s], ["pc" + s], W)
+        ts(un(k, u), pe(u), 0.0, None, ALU.max, None, ["pc" + s], [k + s], W)
+        mms([(pc(u), T.IDh[:], T.MKl[:, 0:W], True, False)], ["IDh", "MKl"], ["pc" + s], W)
+        tt(un("sA", u), un(k, u), un("AT", u), ALU.mult, [k + s, "AT" + s], ["sA" + s], W, 2)
+        mms([(pc(u), T.BOh[:], un("sA", u), False, True)], ["BOh", "sA" + s], ["pc" + s], W)
+        scn(un("sc", u), pc(u), W, ["pc" + s], ["sc" + s])
+        ts(tab("NL", u), last16("sc", u), float(B - 1), None, ALU.add, None, ["sc" + s], ["NL" + s], WB)
+
+    def advance(t, u):
+        s = str(u)
+        tt(un("s", u), xw(t).indirect(tab("NL", u)), un("z", u), ALU.add, XK + ["NL" + s, "z" + s], ["s" + s], W, 1, GAT)
+        act(un("z", u), un("s", u), ACT.Identity, 79.75, 0.5, ["s" + s], ["z" + s], W)
+
+    peers = [T.cores[q] for q in range(len(T.cores)) if q != rank]
+
+    def finish(t, u):
+        s = str(u)
+        act(un("yg", u), xw(t).indirect(tab("NL", u)), ACT.Identity, 160.0, 1.0, XK + ["NL" + s], ["yg" + s], W, GAT)
+        mms([(pe(u), T.BOh[:], un("sA", u), True, True)], ["BOh", "sA" + s], ["pc" + s], W)
+        cp(un("vb", u), pe(u), ["pc" + s], ["vb" + s], W)
+        ts(tab("vT", u), last16("sc", u), float(-CEN - 1), None, ALU.add, None, ["sc" + s], ["vT" + s], WB)
+        ts(tab("vX", u), last16("sc", u), float(B + CEN), None, ALU.add, None, ["sc" + s], ["vX" + s], WB)
+        tt(un("gt", u), un("yg", u), un("z", u), ALU.is_gt, ["yg" + s, "z" + s], ["gt" + s], W, 2)
+        mms([(pc(u), T.IDh[:], T.MK0[:, 0:W], True, False)], ["IDh", "MK0"], ["pc" + s], W)
+        mms([(pc(u), T.BOb[:], un("gt", u), False, True)], ["BOb", "gt" + s], ["pc" + s], W)
+        scn(un("sv", u), pc(u), W, ["pc" + s], ["sv" + s])
+        ts(tab("wt", u), last16("sv", u), 9.0, 2.0 ** -9, ALU.is_lt, ALU.add, ["sv" + s], ["wt" + s], WB)
+        tt(un("s2", u), un("yg", u), un("z", u), ALU.add, ["yg" + s, "z" + s], ["s2" + s], W, 2)
+        act(un("z", u), un("s2", u), ACT.Identity, -0.25, 0.5, ["s2" + s], ["z" + s], W)
+        for b in range(W // 64):
+            q = W // 64 * u + b
+            d = (q - rank) % len(T.cores)
+            zz = T.z[:, 64 * q:64 * q + 64]
+            if d == 0:
+                c0 = B + W0N + K * t + 64 * rank
+                act(T.X[:, c0:c0 + 64], zz, ACT.Identity, -160.0, 1.0, ["z" + s], ["Xo%d" % t], 64)
+            else:
+                k = q if q < rank else q - 1
+                pp = T["pc" + s][:, 64 * b:64 * b + 64]
+                mms([(pp, T["PM%d" % d][:], zz, True, True)], ["PM%d" % d, "z" + s], ["pc" + s], 64)
+                act(T.snd[:, 64 * k:64 * k + 64], pp, ACT.Identity, -160.0, 1.0, ["pc" + s], ["snd%d" % k], 64)
+
+    def send(t):
+        used = []
+        trs = [None] * len(peers)
+        c0 = B + W0N + K * t + 64 * rank
+        for k in sorted(range(len(peers)), key=lambda k: topo.chip(peers[k]) == topo.chip(core)):
+            en = [e for e in topo.engines(core, peers[k]) if e not in used][:4]
+            used += en
+            rid, pid = topo.addr(peers[k])[:2]
+            trs[k] = RemoteDMATransfer(dst_ids=[DstId(rid=rid, pnc=pid)], dma_engine_mask=sum(1 << e for e in en),
+                                       remote_sem=T.sem["arr%d" % t], src=T.snd[:, 64 * k:64 * k + 64], dst=T.X[:, c0:c0 + 64])
+        rec("G", "send", lambda: g.remote_dma_fused(trs, local_sem=T.sem.snt), ["snd%d" % k for k in range(len(peers))],
+            ["Xa%d" % t], 1.5, 4.0, "arr%d" % t)
+
+    def pairs(k, c0, c1):
+        u = k // WB
+        ts(T.EQ[:, 256 * k + c0:256 * k + c1], T.vb[:, c0:c1], T.vT[:, k:k + 1], T.wt[:, k:k + 1], ALU.is_equal, ALU.mult,
+           ["vb%d" % v for v in range(c0 // W, c1 // W)] + ["vT%d" % u, "wt%d" % u], ["EQ%d_%d" % (k, c0)], c1 - c0, 0.5)
+
+    def sums(ps, k, c0, c1, mats, last=False):
+        a, b = 16 * k, 16 * k + 16
+        lst = []
+        nn = 0
+        for lo, hi, m in ((c0, min(a, c1), "FBb"), (a, b, "MTb"), (max(b, c0), c1, "NBb")):
+            if lo < hi and lo >= c0 and hi <= c1 and m in mats:
+                lst.append((T[ps][:, lo:hi], T[m][:], T.EQ[:, 256 * k + lo:256 * k + hi], False, last))
+                nn += max(64, hi - lo)
+        if lst:
+            mms(lst, list(mats) + ["EQ%d_%d" % (k, c0)], [ps], nn / len(lst))
+
+    def joint(u):
+        s = str(u)
+        if u == 0:
+            mms([(T.pd0[:, 0:256], T.IDh[:], T.MKl[:], True, False), (T.pd0[:, 0:256], T.IDh[:], T.MK2[:], False, False)],
+                ["IDh", "MKl", "MK2"], ["pd0"], 256)
+        mms([(T.pd0[:, W * u:W * u + W], T.BOh[:], un("sA", u), False, False)], ["BOh", "sA" + s], ["pd0"], W)
+        for k in range(WB * u):
+            pairs(k, W * u, W * u + W)
+            sums("pd0", k, W * u, W * u + W, ("NBb",))
+        for k in range(WB * u, WB * u + WB):
+            pairs(k, 0, W * u + W)
+            if u < NU - 1:
+                sums("pd0", k, 0, W * u + W, ("FBb", "MTb", "NBb"))
+            else:
+                sums("pd0", k, 0, K, ("MTb", "NBb"), k == 15)
+
+    def settle(t):
+        f = T.scL[:, 15:256:16]
+        scn(T.scL[:], T.pd0[:, 0:256], 256, ["pd0"], ["scL"])
+        if t < RO - 1:
+            tt(T.ofs[:], f, T.TR[:], ALU.max, ["scL", "TR"], ["ofs"], 16, 2)
+            cp(T.OFF[:], T.ofs[:], ["ofs"], ["OFF"], 16)
+            cp(aw(t).indirect(T.OFF[:]), T.VA[:], ["VA", "OFF"], AK, 256, 3.0)
+        stage[0] = 20 * t + 17.5
+        mms([(T.pd1[:, 0:256], T.IDh[:], T.MKl[:], True, False)], ["IDh", "MKl"], ["pd1"], 256)
+        for k in range(16 - WB, 16):
+            sums("pd1", k, 0, 256, ("FBb",), k == 15)
+        tt(T.fd[:], f, T.vX[:], ALU.subtract, ["scL"] + ["vX%d" % u for u in range(NU)], ["fd"], 16, 2)
+        scn(T.scM[:], T.pd1[:, 0:256], 256, ["pd1"], ["scM"])
+        tt(T.fe[:], T.fd[:], T.scM[:, 15:256:16], ALU.add, ["fd", "scM"], ["fe"], 16, 2)
+        ts(T.ff[:], T.fe[:], 0.0007, None, ALU.is_lt, None, ["fe"], ["ff"], 16)
+        tt(T.fm[:], T.ff[:], f, ALU.mult, ["ff", "scL"], ["fm"], 16, 2)
+        tt(T.fo[:], T.fm[:], T.TR[:], ALU.max, ["fm", "TR"], ["fo"], 16, 2)
+        cp(T.OFX[:], T.fo[:], ["fo"], ["OFX"], 16)
+        cp(xw(t).indirect(T.OFX[:]), T.VX[:], ["VX", "OFX"], XK, 256, 3.0)
+
+    def newlinks(t):
+        ts(T.AF[:], aw(t).indirect(T.NL[:]), col("nr%d" % t), None, ALU.mult, None,
+           AK + ["NL%d" % u for u in range(NU)] + ["cnr%d" % t], ["AF"], 256, 1, GAT)
+        tt(T.VA[:], T.AF[:], T["NW%d" % t][:], ALU.add, ["AF", "NW%d" % t], ["VA"], 256, 2)
+        c0 = B + W0N + K * t
+        ts(T.A[:, c0:c0 + K], T.AF[:], col("m15"), col("m15m"), ALU.mult, ALU.add, ["AF", "cm15", "cm15m"], ["An%d" % t], 256)
+
+    for t in range(RO):
+        for u in range(NU):
+            stage[0] = 20 * t + 1 + u
+            s = str(u)
+            act(un("z", u), xw(max(t - 1, 0)).indirect(tab("NL", u)), ACT.Identity, 160.0, 1.0, XK + ["NL" + s], ["z" + s], W, GAT)
+            prep(t, u)
+        if t:
+            XK = XK + ["Xa%d" % (t - 1), "Xo%d" % (t - 1)]
+        for st in range(S):
+            for u in range(NU):
+                stage[0] = 20 * t + 1 + NU * st + u
+                bulk(t, u, st)
+                choose(t, u, st)
+                if st < S - 1:
+                    prep(t, u)
+                    advance(t, u)
+                else:
+                    finish(t, u)
+                    stage[0] = 20 * t + 16.5
+                    joint(u)
+        stage[0] = 20 * t + 17
+        send(t)
+        act(T.VX[:], T.yg[:], ACT.Identity, col("fb"), col("fs"), ["yg%d" % u for u in range(NU)] + ["cfb", "cfs"], ["VX"], 256)
+        if t < RO - 1:
+            newlinks(t)
+        else:
+            ts(T.vout[:], T.vb[:], float(CEN), None, ALU.add, None, ["vb%d" % u for u in range(NU)], ["vout"], 256)
+            dma("Y", T.yv[:], T.vout[0:128:16, :], "dO", ["vout"], [], 2.0)
+        settle(t)
+        if t < RO - 1:
+            AK = AK + ["An%d" % t]
+    XK = XK + ["Xa%d" % (RO - 1), "Xo%d" % (RO - 1)]
+    dma("Y", T.yx[:], T.X[:, B:B + W0N + RO * K], "dO", XK, [], 5.0)
+
+    n = len(recs)
+    preds = [set() for _ in range(n)]
+    lw, lr = {}, {}
+
+    def bank(k):
+        return k[0] == "p"
+
+    for i, r in enumerate(recs):
+        reads, writes = r[3], r[4]
+        for k in reads:
+            if k in lw:
+                preds[i].add(lw[k])
+            lr.setdefault(k, []).append(i)
+        for k in writes:
+            if k in lw:
+                preds[i].add(lw[k])
+            preds[i].update(lr.get(k, []))
+        for k in reads + writes:
+            if bank(k) or k in writes:
+                lw[k] = i
+                lr[k] = []
+        preds[i].discard(i)
+    succ = [[] for _ in range(n)]
+    for i in range(n):
+        for j in preds[i]:
+            succ[j].append(i)
+    prio = [0.0] * n
+    for i in range(n - 1, -1, -1):
+        prio[i] = recs[i][5] + recs[i][6] + max([prio[j] + WK for j in succ[i]], default=0.0)
+    left = [len(p) for p in preds]
+    ready = [0.0] * n
+    avail = {q: [] for q in QUE}
+    for i in range(n):
+        if left[i] == 0:
+            avail[recs[i][0]].append(i)
+    tq = {q: 0.0 for q in QUE}
+    order = []
+    while len(order) < n:
+        best = None
+        for q in QUE:
+            if avail[q]:
+                e = min(max(tq[q], ready[i]) for i in avail[q])
+                if best is None or e < best[0]:
+                    best = (e, q)
+        e, q = best
+        c = [i for i in avail[q] if max(tq[q], ready[i]) <= e + LOOK]
+        i = max(c, key=lambda j: (-recs[j][8], prio[j], -j))
+        avail[q].remove(i)
+        tq[q] = max(tq[q], ready[i]) + recs[i][5]
+        end = tq[q] + recs[i][6]
+        order.append(i)
+        for j in succ[i]:
+            same = recs[j][0] == q == "P"
+            ready[j] = max(ready[j], tq[q] if same else end + WK)
+            left[j] -= 1
+            if left[j] == 0:
+                avail[recs[j][0]].append(j)
+
+    cnt = {}
+    known = {q: {} for q in QUE}
+    lastw, lastr = {}, {}
+
+    def need(q, tok):
+        sem, val, clk = tok
+        kn = known[q]
+        if kn.get(sem, 0) >= val:
+            return
+        QUE[q].wait_ge(T.sem[sem], val)
+        kn[sem] = val
+        for s_, v_ in clk.items():
+            if kn.get(s_, 0) < v_:
+                kn[s_] = v_
+
+    total = {}
+    for r in recs:
+        if r[1] == "dma":
+            total[r[7]] = total.get(r[7], 0) + 16
+    for i in order:
+        q, kind, fn, reads, writes, dur, lat, sem, stg = recs[i]
+        toks = []
+        for k in reads:
+            if bank(k):
+                toks += [x for q2, x in lastr.get(k, {}).items() if q2 != q]
+            elif k in lastw:
+                toks.append(lastw[k])
+        for k in writes:
+            if k in lastw:
+                toks.append(lastw[k])
+            toks += [x for q2, x in lastr.get(k, {}).items() if q2 != q or not bank(k)]
+        for x in sorted(toks, key=lambda x: -x[1]):
+            need(q, x)
+        if kind == "op":
+            sm = "q" + q
+            cnt[sm] = cnt.get(sm, 0) + 1
+            fn().then_inc(T.sem[sm], 1)
+            tok = rtok = (sm, cnt[sm], dict(known[q]))
+            who = q
+        elif kind == "dma":
+            fn().then_inc(T.sem[sem], 16)
+            cnt[sem] = total[sem]
+            tok = rtok = (sem, total[sem], dict(known[q]) if total[sem] == 16 else {})
+            who = q + sem
+        else:
+            fn()
+            cnt["snt"] = cnt.get("snt", 0) + 4 * len(peers)
+            rtok = ("snt", cnt["snt"], dict(known[q]))
+            cnt[sem] = 4 * len(peers)
+            tok = (sem, cnt[sem], {})
+            who = "rem"
+        for k in writes:
+            if bank(k):
+                lastr.setdefault(k, {})[q] = tok
+            else:
+                lastw[k] = tok
+                lastr[k] = {}
+        for k in reads:
+            lastr.setdefault(k, {})[who] = rtok
+    for sem, val in cnt.items():
+        need("Y", (sem, val, {}))

@@ -11,16 +11,23 @@ W = K // NU
 WB = W // 16
 B = 272
 CEN = 1919
-NM = 15
-GC = 7
-MC = 256 // W
+LOW = 2048
+LIFT = 4096
+HOLD = 8192
+PG = 4
+CUT = (1, 8)
+ZQ = "V"
+FINE = True
 XC = B + W0N + RO * K
 AC = B + W0N + (RO - 1) * K
 CYC = 0.00083
-PEC = 0.00045
-GAT = 1.4
-WK = 0.2
+PEC = 0.00042
+GAT = 1.45
+SCA = 3.8
+WK = 0.26
 LOOK = 0.02
+LATE = 12
+ENG = 4
 
 SCRATCH = {}
 
@@ -32,42 +39,44 @@ def _b(name, cols, dtype, where="sbuf"):
 _b("X", XC, "bfloat16")
 _b("A", AC, "int32")
 _b("WL", 16, "int32")
-for _n in ("NL", "OFF", "OFX"):
+for _n in ("OFA", "OFX"):
     _b(_n, 16, "uint16")
-for _n in ("z", "ok", "s", "gt", "yg", "sel0", "sel1", "sel2", "sel3", "VX"):
+for _n in ("z", "zt", "ok", "gt", "yg", "VX", "cT", "J", "JM", "ta", "tb", "tc", "td", "te", "tf"):
     _b(_n, 256, "bfloat16")
-for _n in ("AT", "T1", "sA", "vb", "MKl", "MK2"):
+for _n in ("AT", "T1", "sA0", "sA1", "sA2", "sA3", "vb", "MK0", "NW0", "NW1"):
     _b(_n, 256, "float16")
 _b("LT", 256, "uint16")
-_b("xg", 15 * 256, "bfloat16")
-_b("mn", 15 * 256, "bfloat16")
+_b("xg0", 16 * 256, "bfloat16")
+_b("xg1", 16 * 256, "bfloat16")
+_b("mn", 16 * 256, "bfloat16")
 for _u in range(NU):
     _b("pd%d" % _u, 512, "float32", "psum")
     _b("pc%d" % _u, 512, "float32", "psum")
-for _n in ("vT", "vX", "wt", "ofs", "fd", "fe", "ff", "fm", "fo", "TR"):
+for _n in ("vT", "wt", "vX", "fe", "fm", "fo"):
     _b(_n, 16, "float32")
 _b("EQ", 16 * 256, "bfloat16")
-for _n in ("sc", "sv", "s2", "scL", "scM", "AF", "VA", "vout", "J", "JM", "ta", "tb", "tc", "td", "RS", "NW0", "NW1"):
+for _n in ("sc", "sv", "scX", "VA", "vout", "JC", "D0"):
     _b(_n, 256, "float32")
+_b("M", W, "float32")
 _b("snd", 192, "bfloat16")
-_b("PI", 4, "int32")
-_b("col", 32, "float32")
-_b("JG", 128, "float32")
-_b("JP", 128, "float32")
-_b("W1", 144, "bfloat16")
-_b("W2", 144, "bfloat16")
-for _n in ("BOb", "NBb", "FBb", "MTb", "ZS", "DEAD", "TRI0", "TRI1", "TRI2", "IDb", "PM1", "PM2", "PM3"):
+_b("PI", 8, "int32")
+_b("PJ", 16, "float32")
+_b("col", 64, "float32")
+_b("W1", 248, "bfloat16")
+_b("W2", 248, "bfloat16")
+for _n in ("JG", "JE", "J8", "BOb", "NB", "FB", "MT", "FS", "MS", "ZS", "TRI0", "TRI1", "TRI2", "PH0", "PH1", "PH2", "PH3"):
     _b(_n, 128, "bfloat16")
-for _n in ("BOh", "IDh", "SW00", "SW01", "SW10", "SW11", "MK0"):
+for _n in ("BOh", "IDh", "PAT", "DEAD", "SW00", "SW01", "SW10", "SW11", "RW0", "RW1"):
     _b(_n, 128, "float16")
 
-SEMAPHORES = ["qV", "qS", "qP", "qG", "dX", "dW", "dA", "dO", "arr0", "arr1", "arr2", "snt"]
+SEMAPHORES = ["qV", "qS", "qP", "qG", "dX", "dW", "dA", "dO", "dE", "arr0", "arr1", "arr2", "snt"]
 
 
 def rank_program(g, core, T, topo):
     rank = T.rank_of(core)
     if rank is None:
         return
+    NR = len(T.cores)
     QUE = {"V": g.vector, "S": g.scalar, "P": g.tensor, "G": g, "Y": g.sync}
     recs = []
     stage = [0]
@@ -99,9 +108,6 @@ def rank_program(g, core, T, topo):
     def act(out, in_, f, bias, scale, reads, writes, n=128, ind=1.0):
         op("S", lambda: g.scalar.activation(out, in_, f, bias=bias, scale=scale), reads, writes, 0.065 + n * CYC * ind)
 
-    def scn(out, data1, n, reads, writes):
-        op("V", lambda: g.vector.tensor_tensor_scan(out, T.RS[:, 0:n], data1, 0.0, ALU.mult, ALU.max), ["RS"] + reads, writes, vd(n))
-
     def mms(lst, reads, writes, n=128):
         def go():
             r = None
@@ -110,11 +116,15 @@ def rank_program(g, core, T, topo):
             return r
         op("P", go, reads, writes, len(lst) * max(n, 64) * PEC)
 
-    dma("Y", T.WL[:], T.w0[:], "dW", [], ["WL"], 2.0)
-    dma("Y", T.X[:, B:B + W0N], T.x0[:], "dX", [], ["X"], 5.0)
+    stage[0] = -1
+    dma("Y", T.WL[:], T.w0[:], "dW", [], ["WL"], 3.0)
+    stage[0] = 0
+    dma("S", T.A[15:128:16, B:B + W0N], T.nx[:], "dA", [], ["A8"], 6.0)
     for gr in range(8):
-        dma("S" if gr % 2 == 0 else "Y", T.A[16 * gr:16 * gr + 15, B:B + W0N], T.lk[16 * gr:16 * gr + 15, :], "dA", [], ["A%d" % gr], 9.0)
-    dma("S", T.A[15:128:16, B:B + W0N], T.nx[:], "dA", [], ["A8"], 9.0)
+        dma("S" if gr % 2 else "Y", T.A[16 * gr:16 * gr + 15, B:B + W0N], T.lk[16 * gr:16 * gr + 15, :], "dA", [], ["A%d" % gr], 6.0)
+    stage[0] = 0.1
+    dma("Y", T.X[:, B:B + W0N], T.x0[:], "dX", [], ["X"], 7.5)
+    stage[0] = 0
     AK = ["A%d" % i for i in range(9)] + ["Am"]
     XK = ["X", "Xm"]
 
@@ -125,6 +135,9 @@ def rank_program(g, core, T, topo):
         return col(name)
 
     def col(name):
+        if name[0] == "P":
+            i = int(name[1:]) // 16 + 7
+            return T.PJ[:, i:i + 1]
         i = CI[name]
         return T.col[:, i:i + 1]
 
@@ -134,85 +147,115 @@ def rank_program(g, core, T, topo):
         else:
             op("G", lambda: g.iota(ap, pattern, base, cm, allow_small_or_imprecise_dtypes=True), [], [key], 0.13 + 2 * CYC * n)
 
-    iota(T.PI[:, 0:1], "PI", [[0, 1]], 0, 1, 1, True)
-    iota(T.JG[:], "JG", [[16, 8], [0, 16]], 0, 0, 128)
+    def ck(name):
+        return "PJ" if name[0] == "P" else "c" + name
+
+    def mkcol(name, src, s1, s2, op0, op1):
+        in0, key = (T.PI[:, src:src + 1], "PI%d" % src) if isinstance(src, int) else (col(src), ck(src))
+        rd = [key] + [ck(s) for s in (s1, s2) if isinstance(s, str)]
+        ts(newcol(name), in0, col(s1) if isinstance(s1, str) else s1, col(s2) if isinstance(s2, str) else s2, op0, op1, rd, ["c" + name], 1)
+
+    def mat(out, src, s1, s2, op0, op1, n=128):
+        rd = [src] + [ck(s) for s in (s1, s2) if isinstance(s, str)]
+        ts(T[out][:, 0:n], T[src][:, 0:n], col(s1) if isinstance(s1, str) else s1, col(s2) if isinstance(s2, str) else s2,
+           op0, op1, rd, [out], n, 0.5)
+
+    def mat2(out, a, b, o, n=128, f=1.0):
+        tt(T[out][:, 0:n], T[a][:, 0:n], T[b][:, 0:n], o, [a, b], [out], n, f)
+
+    def lst_(u, a, b):
+        return T.LT[:, 16 * WB * u + WB * a:16 * WB * u + WB * b]
+
+    iota(T.PI[:, 0:1], "PI0", [[0, 1]], 0, 1, 1, True)
+    iota(T.PJ[:], "PJ", [[16, 16]], -112, 1, 16)
     iota(T.J[:], "J", [[1, 256]], 0, 0, 256)
+    iota(T.J8[:], "J8", [[0, 16], [16, 8]], 0, 0, 128)
+    iota(T.JE[:], "JE", [[1, 2], [2, 8], [0, 8]], 0, 0, 128)
+    iota(T.JG[:], "JG", [[16, 8], [0, 16]], 0, 0, 128)
     iota(T.JM[:], "JM", [[0, 16], [1, 16]], 0, 0, 256)
-
-    def mkcol(name, in0, s1, s2, op0, op1, reads):
-        ts(newcol(name), in0, s1, s2, op0, op1, reads, ["c" + name], 1)
-
-    ts(T.NL[:], T.WL[:], float(B), None, ALU.add, None, ["WL"], ["NL%d" % u for u in range(NU)], 16)
     op("V", lambda: g.vector.memset(T.A[:, 0:B], -1), [], ["Am"], vd(B))
     op("V", lambda: g.vector.memset(T.X[:, 0:B], 95.0), [], ["Xm"], vd(B, 0.5))
-    ts(T.PI[:, 1:2], T.PI[:, 0:1], 15, None, ALU.bitwise_and, None, ["PI"], ["PI1"], 1)
-    ts(T.PI[:, 2:3], T.PI[:, 0:1], 16, None, ALU.bitwise_and, None, ["PI"], ["PI2"], 1)
-    ts(T.PI[:, 3:4], T.PI[:, 0:1], 1, None, ALU.bitwise_and, None, ["PI"], ["PI3"], 1)
-    for n_, a in (("P", 0), ("Pm16", -16), ("Pp16", 16), ("Pp32", 32), ("Pp48", 48), ("Pm112", -112), ("Pm96", -96), ("Pm80", -80)):
-        mkcol(n_, T.PI[:, 0:1], float(a), None, ALU.add, None, ["PI"])
-    mkcol("R", T.PI[:, 1:2], 0.0, None, ALU.add, None, ["PI1"])
-    mkcol("U1", T.PI[:, 2:3], 0.0625, None, ALU.mult, None, ["PI2"])
-    mkcol("U0", T.PI[:, 2:3], -0.0625, 1.0, ALU.mult, ALU.add, ["PI2"])
-    mkcol("fs", T.PI[:, 3:4], 2.0, -1.0, ALU.mult, ALU.add, ["PI3"])
-    mkcol("fb", T.PI[:, 3:4], -335.0, 175.0, ALU.mult, ALU.add, ["PI3"])
-    tt(newcol("G"), col("P"), col("R"), ALU.subtract, ["cP", "cR"], ["cG"], 1)
-    mkcol("G15", col("G"), 15.0, None, ALU.add, None, ["cG"])
-    mkcol("m15", col("R"), 15.0, None, ALU.is_equal, None, ["cR"])
-    mkcol("m15m", col("m15"), -1.0, None, ALU.add, None, ["cm15"])
-    for t in range(RO - 1):
-        mkcol("r%d" % t, col("R"), float(13 + t), None, ALU.is_equal, None, ["cR"])
-        mkcol("nr%d" % t, col("R"), float(13 + t), None, ALU.not_equal, None, ["cR"])
-    mkcol("d128", col("R"), 15.0, 128.0, ALU.is_lt, ALU.mult, ["cR"])
-    mkcol("x16", col("m15"), -16.0, None, ALU.mult, None, ["cm15"])
-    tt(newcol("RP"), col("R"), col("x16"), ALU.add, ["cR", "cx16"], ["cRP"], 1)
-    J1, JM1 = T.J[:, 0:128], T.JM[:, 0:128]
-    for u, h, n_ in ((0, 0, "P"), (1, 1, "P"), (0, 1, "Pp16"), (1, 0, "Pm16")):
-        nm = "SW%d%d" % (u, h)
-        ts(T[nm][:], J1, col(n_), col("U%d" % u), ALU.is_equal, ALU.mult, ["J", "c" + n_, "cU%d" % u], [nm])
-    ts(T.IDb[:], J1, col("P"), None, ALU.is_equal, None, ["J", "cP"], ["IDb"])
-    ts(T.BOb[:], T.JG[:], col("G"), None, ALU.is_equal, None, ["JG", "cG"], ["BOb"])
-    ts(T.ta[:, 0:128], JM1, float(NM), None, ALU.is_lt, None, ["JM"], ["ta0"])
-    tt(T.ZS[:], T.ta[:, 0:128], T.BOb[:], ALU.mult, ["ta0", "BOb"], ["ZS"], 128, 2)
-    ts(T.W1[:], T.J[:, 0:144], col("G15"), None, ALU.is_equal, None, ["J", "cG15"], ["W1"], 144)
-    ts(T.W2[:], T.J[:, 0:144], col("G15"), -2.0, ALU.is_equal, ALU.mult, ["J", "cG15"], ["W2"], 144)
-    ts(T.tb[:, 0:128], JM1, 15.0, -16.0, ALU.is_equal, ALU.mult, ["JM"], ["tb0"])
-    tt(T.JP[:], T.tb[:, 0:128], JM1, ALU.add, ["tb0", "JM"], ["JP"], 128, 2)
-    ts(T.ta[:, 128:256], T.JP[:], col("RP"), -2.0, ALU.is_lt, ALU.mult, ["JP", "cRP"], ["ta1"])
-    ts(T.tb[:, 128:256], T.JP[:], col("RP"), None, ALU.is_equal, None, ["JP", "cRP"], ["tb1"])
-    tt(T.tc[:, 0:128], T.ta[:, 128:256], T.tb[:, 128:256], ALU.add, ["ta1", "tb1"], ["tc0"], 128, 2)
-    tt(T.tc[:, 128:256], T.tc[:, 0:128], T.BOb[:], ALU.mult, ["tc0", "BOb"], ["tc1"], 128, 2)
+    for i, m in ((1, 15), (2, 16), (3, 1), (4, 7), (5, 56), (6, 64)):
+        ts(T.PI[:, i:i + 1], T.PI[:, 0:1], m, None, ALU.bitwise_and, None, ["PI0"], ["PI%d" % i], 1)
+    mkcol("R", 1, 0.0, None, ALU.add, None)
+    mkcol("U1", 2, 0.0625, None, ALU.mult, None)
+    mkcol("U0", 2, -0.0625, 1.0, ALU.mult, ALU.add)
+    mkcol("G", "R", -1.0, "P0", ALU.mult, ALU.add)
+    mkcol("m15", "R", 15.0, None, ALU.is_equal, None)
+    mkcol("g8", 4, 16.0, None, ALU.mult, None)
+    mkcol("e2", 5, 0.25, None, ALU.mult, None)
+    mkcol("E", 6, 1.0 / 64, "e2", ALU.mult, ALU.add)
+    mkcol("e0", "E", 0.0, 1e9, ALU.is_equal, ALU.mult)
+    mkcol("thr0", "e0", 68.0, None, ALU.add, None)
+    for k in range(1, S):
+        mkcol("thr%d" % k, "E", -float(LOW * k), "thr0", ALU.mult, ALU.add)
+    mkcol("R1", "R", 1.0, None, ALU.add, None)
+    mkcol("RE", "m15", -16.0, "R1", ALU.mult, ALU.add)
+    mkcol("r0", "R", 0.0, 2.0 * HOLD, ALU.is_equal, ALU.mult)
+    mkcol("oNL", "r0", float(CEN + B + 15 * LOW - HOLD), None, ALU.add, None)
+    mkcol("Rb", "r0", 8.0 / HOLD, -1.0, ALU.mult, ALU.add)
+    mkcol("Rm", "Rb", "R", None, ALU.add, None)
+    mkcol("e1", "E", 0.0, None, ALU.is_gt, None)
+    for u, h, n_ in ((0, 0, "P0"), (1, 1, "P0"), (0, 1, "P16"), (1, 0, "P-16")):
+        mat("SW%d%d" % (u, h), "J", n_, "U%d" % u, ALU.is_equal, ALU.mult)
+    for u in range(NU):
+        ts(lst_(u, 0, 1), T.WL[:, WB * u:WB * u + WB], float(B), None, ALU.add, None, ["WL"], ["NL%d" % u], WB)
+    mat("ZS", "J8", "G", None, ALU.is_equal, None)
+    mkcol("g120", "G", 0.0625, 120.0, ALU.mult, ALU.add)
+    mat("W1", "J", "g120", None, ALU.is_equal, None, 248)
+    mat("W2", "J", "g120", -2.0, ALU.is_equal, ALU.mult, 248)
+    mat("ta", "JE", "RE", None, ALU.is_equal, None)
+    mat2("PAT", "ta", "ZS", ALU.mult)
+    mat("td", "J8", "g8", None, ALU.is_equal, None)
+    mat("ta", "JE", "E", -2.0 * LOW, ALU.is_lt, ALU.mult)
+    mat("tb", "JE", "E", 2.0 * LOW, ALU.is_equal, ALU.mult)
+    mat2("tc", "ta", "tb", ALU.add)
+    mat2("te", "tc", "td", ALU.mult)
     for t in range(RO):
-        nm = "rv%d" % t
-        mkcol(nm, col("RP"), float(13 + t), None, ALU.is_lt, None, ["cRP"])
-        ts(T.td[:, 0:128], T.JP[:], float(13 + t), col(nm), ALU.is_lt, ALU.mult, ["JP", "c" + nm], ["td0"])
-        tt(T["TRI%d" % t][:], T.td[:, 0:128], T.tc[:, 128:256], ALU.mult, ["td0", "tc1"], ["TRI%d" % t], 128, 2)
-    ts(T.BOh[:], T.JG[:], col("G"), None, ALU.is_equal, None, ["JG", "cG"], ["BOh"])
-    ts(T.IDh[:], J1, col("P"), None, ALU.is_equal, None, ["J", "cP"], ["IDh"])
-    ts(T.ta[:], T.JM[:], col("R"), 8192.0 + CEN + 1, ALU.is_equal, ALU.mult, ["JM", "cR"], ["ta0", "ta1"], 256)
-    ts(T.MKl[:], T.ta[:], -8192.0, None, ALU.add, None, ["ta0", "ta1"], ["MKl"], 256)
-    ts(T.RS[:], T.JM[:], 0.0, None, ALU.is_gt, None, ["JM"], ["RS"], 256)
-    ts(T.tb[:, 0:128], JM1, col("R"), col("d128"), ALU.is_ge, ALU.mult, ["JM", "cR", "cd128"], ["tb0"])
-    ts(T.tb[:, 128:256], JM1, 15.0, None, ALU.is_lt, None, ["JM"], ["tb1"])
-    tt(T.tc[:, 0:128], T.tb[:, 0:128], T.tb[:, 128:256], ALU.mult, ["tb0", "tb1"], ["tc0"], 128, 2)
-    tt(T.DEAD[:], T.tc[:, 0:128], T.BOb[:], ALU.mult, ["tc0", "BOb"], ["DEAD"], 128, 2)
-    stage[0] = 5
-    ts(T.tb[:, 128:256], JM1, col("R"), 8192.0, ALU.is_equal, ALU.mult, ["JM", "cR"], ["tb1"])
-    ts(T.MK0[:], T.tb[:, 128:256], -8192.0, None, ALU.add, None, ["tb1"], ["MK0"])
-    ts(T.MK2[:], T.JM[:], col("R"), float(B - 1), ALU.is_equal, ALU.mult, ["JM", "cR"], ["MK2"], 256)
-    ts(T.NBb[:], T.JG[:], col("G"), -float(2 ** 23), ALU.is_equal, ALU.mult, ["JG", "cG"], ["NBb"])
-    ts(T.FBb[:], T.JG[:], col("G"), 2.0 ** -10, ALU.is_equal, ALU.mult, ["JG", "cG"], ["FBb"])
-    ts(T.ta[:, 0:128], JM1, col("R"), -float(2 ** 23), ALU.is_gt, ALU.mult, ["JM", "cR"], ["ta0"])
-    ts(T.ta[:, 128:256], JM1, col("R"), 2.0 ** -10, ALU.is_le, ALU.mult, ["JM", "cR"], ["ta1"])
-    tt(T.td[:, 128:256], T.ta[:, 0:128], T.ta[:, 128:256], ALU.add, ["ta0", "ta1"], ["td1"], 128, 2)
-    tt(T.MTb[:], T.td[:, 128:256], T.BOb[:], ALU.mult, ["td1", "BOb"], ["MTb"], 128, 2)
-    for d, n1, n2 in (("1", "Pp16", "Pm112"), ("2", "Pp32", "Pm96"), ("3", "Pp48", "Pm80")):
-        ts(T.ta[:, 0:128], J1, col(n1), None, ALU.is_equal, None, ["J", "c" + n1], ["ta0"])
-        ts(T.tb[:, 0:128], J1, col(n2), None, ALU.is_equal, None, ["J", "c" + n2], ["tb0"])
-        tt(T["PM" + d][:], T.ta[:, 0:128], T.tb[:, 0:128], ALU.add, ["ta0", "tb0"], ["PM" + d], 128, 2)
+        stage[0] = LATE if t else 0
+        mkcol("rv%d" % t, "E", float(14 + t), None, ALU.is_lt, None)
+        mat("tf", "JE", float(14 + t), "rv%d" % t, ALU.is_lt, ALU.mult)
+        mat2("TRI%d" % t, "tf", "te", ALU.mult)
+    stage[0] = 0
+    mat("BOh", "JG", "g8", None, ALU.is_equal, None)
+    mat("ta", "JM", "R", float(HOLD), ALU.is_equal, ALU.mult, W)
+    mat("tb", "JM", "Rm", -2.0 * HOLD, ALU.is_equal, ALU.mult, W)
+    mat2("M", "ta", "tb", ALU.add, W, 2)
+    mat("tc", "JE", "E", "e1", ALU.is_ge, ALU.mult)
+    mat2("DEAD", "tc", "td", ALU.mult)
+    HALF = 127.0 / 256
+    mat("PH0", "J", "P0", HALF, ALU.is_equal, ALU.mult)
+    stage[0] = LATE
+    iota(T.JC[:], "JC", [[-16, 16], [0, 16]], 240 - CEN - B + LIFT, 0, 256)
+    mkcol("fs", 3, 2.0, -1.0, ALU.mult, ALU.add)
+    mkcol("fb", 3, -335.0, 175.0, ALU.mult, ALU.add)
+    mkcol("nw15", "m15", CEN + 1.0, -1.0, ALU.mult, ALU.add)
+    mkcol("ovT", "r0", float(15 * LOW - HOLD), None, ALU.add, None)
+    mkcol("oLL", "r0", float(CEN + B - HOLD), None, ALU.add, None)
+    mkcol("ovo", "r0", -1.0, 9.0 + HOLD, ALU.mult, ALU.add)
+    mat("BOb", "JG", "G", None, ALU.is_equal, None)
+    mat("IDh", "J", "P0", None, ALU.is_equal, None)
+    for d in range(1, NR):
+        mat("ta", "J", "P%d" % (16 * d), HALF, ALU.is_equal, ALU.mult)
+        mat("tb", "J", "P%d" % (16 * d - 128), HALF, ALU.is_equal, ALU.mult)
+        mat2("PH%d" % d, "ta", "tb", ALU.add)
+    mat("ta", "JM", "R", 2.0 * LIFT, ALU.is_equal, ALU.mult, 256)
+    mat("MK0", "ta", -float(LIFT), None, ALU.add, None, 256)
+    mat("NB", "JG", "G", -2.0 ** 43, ALU.is_equal, ALU.mult)
+    mat("FB", "JG", "G", -2.0 ** 13, ALU.is_equal, ALU.mult)
+    mat("FS", "JG", "G", -2.0 ** -10, ALU.is_equal, ALU.mult)
+    mat("ta", "JM", "R", None, ALU.is_gt, None)
+    mat2("tb", "ta", "NB", ALU.mult)
+    mat2("MT", "tb", "FB", ALU.min)
+    mat2("MS", "tb", "FS", ALU.min)
+    mat("ta", "JM", 0.0, 2.0 ** 30, ALU.is_gt, ALU.mult, 256)
+    ts(T.JC[:], T.JC[:], col("R"), None, ALU.add, None, ["JC", "cR"], ["JC"], 256)
+    mat2("D0", "ta", "JC", ALU.add, 256, 2)
     for t in range(RO - 1):
-        ts(T["NW%d" % t][:], T.J[:], float(W0N + K * t), col("r%d" % t), ALU.add, ALU.mult, ["J", "cr%d" % t], ["NW%d" % t], 256)
-    ts(T.tb[:, 128:144], T.J[:, 0:16], 16.0, None, ALU.mult, None, ["J"], ["tb1"], 16)
-    ts(T.TR[:], T.tb[:, 128:144], col("R"), None, ALU.add, None, ["tb1", "cR"], ["TR"], 16)
+        mkcol("rt%d" % t, "R", float(13 + t), None, ALU.is_equal, None)
+        mkcol("va%d" % t, "rt%d" % t, 2048.0, float(CEN), ALU.mult, ALU.add)
+        mat("NW%d" % t, "J", float(W0N + K * t + 1 - 2048), "rt%d" % t, ALU.add, ALU.mult, 256)
+        mat("RW%d" % t, "JG", "G", "rt%d" % t, ALU.is_equal, ALU.mult)
 
     def un(name, u):
         return T[name][:, W * u:W * u + W]
@@ -223,14 +266,11 @@ def rank_program(g, core, T, topo):
     def last16(name, u):
         return T[name][:, W * u + 15:W * u + W:16]
 
-    def pz(u, n):
-        return T["pc%d" % u][:, 0:n]
+    def reg(u, k):
+        return T["pc%d" % u][:, W * k:W * k + W]
 
-    def pe(u):
-        return T["pc%d" % u][:, 256:256 + W]
-
-    def pc(u):
-        return T["pc%d" % u][:, 384:384 + W]
+    def xgp(step, u, a, b):
+        return T["xg%d" % (step % 2)][:, 16 * W * u + W * a:16 * W * u + W * b]
 
     def xw(t):
         return T.X[:, 0:B + W0N + K * t]
@@ -238,206 +278,241 @@ def rank_program(g, core, T, topo):
     def aw(t):
         return T.A[:, 0:B + W0N + K * t]
 
+    def own(out, u, k):
+        s = str(u)
+        op("V", lambda: g.vector.tensor_tensor_scan(un(out, u), reg(u, k), T.M[:], -1e6, ALU.max, ALU.add), ["M", "pc" + s], [out + s], vd(W))
+
+    def links(t, u):
+        s = str(u)
+        ts(un("AT", u), aw(t).indirect(lst_(u, 0, 1)), float(-CEN), None, ALU.add, None, AK + ["NL" + s], ["AT" + s], W, 1, GAT)
+
     def prep(t, u):
         s = str(u)
-        ts(un("AT", u), aw(t).indirect(tab("NL", u)), float(-CEN), None, ALU.add, None, AK + ["NL" + s], ["AT" + s], W, 1, GAT)
+        links(t, u)
         nb = W // 32
         o = W * u
         for b in range(nb):
-            op("V", lambda b=b: g.vector.transpose(T.T1[:, o + b:o + W:nb] if nb > 1 else T.T1[:, o:o + W],
-                                                   T.AT[:, o + 32 * b:o + 32 * b + 32]), ["AT" + s], ["T1%s%d" % (s, b)], vd(32))
+            op("V", lambda b=b: g.vector.transpose(T.T1[:, o + b:o + W:nb], T.AT[:, o + 32 * b:o + 32 * b + 32]),
+               ["AT" + s], ["T1%s%d" % (s, b)], vd(32))
         lst = []
         for v in range(2):
             for h in range(2):
-                lst.append((T["pc" + s][:, 384 + v:384 + W:2], T["SW%d%d" % (v, h)][:],
+                lst.append((T["pc" + s][:, W + v:2 * W:2], T["SW%d%d" % (v, h)][:],
                             T.T1[:, o + W // 2 * h:o + W // 2 * h + W // 2], h == 0, h == 1))
         mms(lst, ["T1%s%d" % (s, b) for b in range(nb)] + ["SW00", "SW01", "SW10", "SW11"], ["pc" + s], W // 2)
         n = WB * (13 + t)
-        ts(T.LT[:, o:o + n], T["pc" + s][:, 384:384 + n], float(CEN + B), None, ALU.add, None, ["pc" + s], ["LT" + s], n)
+        ts(lst_(u, 1, 14 + t), T["pc" + s][:, W:W + n], float(CEN + B), None, ALU.add, None, ["pc" + s], ["LT" + s], n)
 
-    def bulk(t, u, step):
+    def newlist(t, u):
+        s = str(u)
+        links(t, u)
+        mms([(reg(u, 6), T["RW%d" % t][:], un("AT", u), True, True)], ["RW%d" % t, "AT" + s], ["pc" + s], W)
+        own("sv", u, 6)
+        ts(lst_(u, 14 + t, 15 + t), last16("sv", u), col("oLL"), None, ALU.add, None, ["sv" + s, "coLL"], ["LL" + s], WB)
+
+    def halve(out, u, d, y, ykey, z, zkey, okey):
+        s = str(u)
+        mms([(reg(u, 0), T["PH%d" % d][:], z, True, False), (reg(u, 0), T["PH%d" % d][:], y, False, True)],
+            ["PH%d" % d, ykey, zkey], ["pc" + s], W)
+        if ZQ == "V" and okey[0:2] != "zt":
+            ts(out, reg(u, 0), 1.0, None, ALU.add, None, ["pc" + s], [okey], W)
+        else:
+            act(out, reg(u, 0), ACT.Identity, 1.0, 1.0, ["pc" + s], [okey], W)
+
+    def zap(u, step):
+        return (xgp(0, u, 0, 1), "xw0%d_0" % u) if step == 0 else (un("z", u), "z%d" % u)
+
+    def bulk(t, u, step, old, new):
         s = str(u)
         nl = 13 + t
-        o = 15 * W * u
+        p = step % 2
+        late = step == 0 and t > 0
+        cuts = [0] + list(CUT) + ([nl] if late else []) + [nl + 1]
         pd = T["pd" + s][:, 0:W]
-        mms([(T["pc" + s][:, W * j:W * j + W], T.IDb[:], un("z", u), True, True) for j in range(MC)], ["IDb", "z" + s], ["pc" + s], W)
-        mms([(pd, T.ZS[:], un("z", u), True, False)], ["ZS", "z" + s], ["pd" + s], W)
-        for k in range(step):
-            mms([(pd, T.DEAD[:], un("sel%d" % k, u), False, False)], ["DEAD", "sel%d%s" % (k, s)], ["pd" + s], W)
-        n2 = min(NM, nl)
-        for a in range(0, n2, GC):
-            b = min(a + GC, n2)
-            x = "xg%s%d" % (s, a)
-            act(T.xg[:, o + W * a:o + W * b], xw(t).indirect(T.LT[:, W * u + WB * a:W * u + WB * b]), ACT.Identity, 160.0, 1.0,
-                XK + ["LT" + s], [x], W * (b - a), GAT)
-            for c in range(a, b, MC):
-                d = min(c + MC, b)
-                h = slice(o + W * c, o + W * d)
-                m = "mn%s%d" % (s, c)
-                tt(T.mn[:, h], T.xg[:, h], pz(u, W * (d - c)), ALU.min, [x, "pc" + s], [m], W * (d - c))
-                mms([(pd, T.W1[:, 15 - i:143 - i], T.xg[:, o + W * i:o + W * i + W], False, False) for i in range(c, d)],
-                    ["W1", x], ["pd" + s], W)
-                mms([(pd, T.W2[:, 15 - i:143 - i], T.mn[:, o + W * i:o + W * i + W], False, i == nl - 1) for i in range(c, d)],
-                    ["W2", m], ["pd" + s], W)
-        for i in range(n2, nl):
-            h = slice(o + W * i, o + W * i + W)
-            x, m = "xg%s%d" % (s, i), "mn%s%d" % (s, i)
-            tt(T.xg[:, h], xw(t).indirect(T.LT[:, W * u + WB * i:W * u + WB * i + WB]), un("z", u), ALU.subtract,
-               XK + ["LT" + s, "z" + s], [x], W, 1, GAT)
-            act(T.mn[:, h], T.xg[:, h], ACT.Abs, 160.0, 1.0, [x], [m], W)
-            mms([(pd, T.W1[:, 15 - i:143 - i], T.mn[:, h], False, i == nl - 1)], ["W1", m], ["pd" + s], W)
+
+        def mn(a, b):
+            return T.mn[:, W * (16 * u + a):W * (16 * u + b)]
+        for a, b in zip(cuts, cuts[1:]):
+            isnew = late and a == nl
+            if isnew:
+                newlist(t - 1, u)
+            win, keys = (xw(t - 1), old) if late and not isnew else (xw(t), new)
+            act(xgp(step, u, a, b), win.indirect(lst_(u, a, b)), ACT.Identity, 160.0, 1.0,
+                keys + (["LL" + s] if isnew else ["NL" + s] if b == 1 else ["NL" + s, "LT" + s]), ["xw%d%s_%d" % (p, s, i) for i in range(a, b)], W * (b - a), GAT)
+            if a == 0:
+                if step:
+                    z0, k0 = zap(u, step - 1)
+                    halve(un("z", u), u, 0, xgp(step, u, 0, 1), "xw%d%s_0" % (p, s), z0, k0, "z" + s)
+                z, zk = zap(u, step)
+            for i in range(max(a, 1), b):
+                tt(mn(i, i + 1), xgp(step, u, i, i + 1), z, ALU.min, [zk, "xw%d%s_%d" % (p, s, i)], ["mn%s_%d" % (s, i)], W)
+            if a == 0:
+                mms([(pd, T.DEAD[:], un("sA%d" % k, u), k == 0, False) for k in range(step)] + [(pd, T.ZS[:], z, step == 0, False)],
+                    ["ZS", zk, "DEAD"] + ["sA%d%s" % (k, s) for k in range(step)], ["pd" + s], W)
+            a = max(a, 1)
+            if a < b:
+                mms([(pd, row("W1", i), xgp(step, u, i, i + 1), False, False) for i in range(a, b)],
+                    ["W1"] + ["xw%d%s_%d" % (p, s, i) for i in range(a, b)], ["pd" + s], W)
+            while a < b:
+                d = min(b, a + (PG if a + PG <= nl - 1 else 2 if a + 2 <= nl else 1))
+                mms([(pd, row("W2", i), mn(i, i + 1), False, i == nl) for i in range(a, d)],
+                    ["W2"] + ["mn%s_%d" % (s, i) for i in range(a, d)], ["pd" + s], W)
+                a = d
+
+    def row(name, e):
+        o = 120 - 64 * (e % 2) - 8 * (e // 2)
+        return T[name][:, o:o + 128]
 
     def choose(t, u, step):
         s = str(u)
-        k = "sel%d" % step
-        ts(un("ok", u), T["pd" + s][:, 0:W], 68.0, None, ALU.is_lt, None, ["pd" + s], ["ok" + s], W)
-        mms([(pe(u), T["TRI%d" % t][:], un("ok", u), True, True)], ["TRI%d" % t, "ok" + s], ["pc" + s], W)
-        ts(un(k, u), pe(u), 0.0, None, ALU.max, None, ["pc" + s], [k + s], W)
-        mms([(pc(u), T.IDh[:], T.MKl[:, 0:W], True, False)], ["IDh", "MKl"], ["pc" + s], W)
-        tt(un("sA", u), un(k, u), un("AT", u), ALU.mult, [k + s, "AT" + s], ["sA" + s], W, 2)
-        mms([(pc(u), T.BOh[:], un("sA", u), False, True)], ["BOh", "sA" + s], ["pc" + s], W)
-        scn(un("sc", u), pc(u), W, ["pc" + s], ["sc" + s])
-        ts(tab("NL", u), last16("sc", u), float(B - 1), None, ALU.add, None, ["sc" + s], ["NL" + s], WB)
+        k = "sA%d" % step
+        ts(un("ok", u), T["pd" + s][:, 0:W], col("thr%d" % step), None, ALU.is_lt, None, ["pd" + s, "cthr%d" % step], ["ok" + s], W)
+        mms([(reg(u, 2), T.PAT[:], un("AT", u), True, False), (reg(u, 2), T["TRI%d" % t][:], un("ok", u), False, True)],
+            ["PAT", "AT" + s, "TRI%d" % t, "ok" + s], ["pc" + s], W)
+        ts(un(k, u), reg(u, 2), -2.0 * LOW, -float(LOW), ALU.add, ALU.max, ["pc" + s], [k + s], W)
+        mms([(reg(u, 3), T.BOh[:], un(k, u), True, True)], ["BOh", k + s], ["pc" + s], W)
+        own("sc", u, 3)
+        ts(lst_(u, 0, 1), last16("sc", u), col("oNL"), None, ALU.add, None, ["sc" + s, "coNL"], ["NL" + s], WB)
 
-    def advance(t, u):
+    peers = [T.cores[q] for q in range(NR) if q != rank]
+
+    def finish(t, u, keys):
         s = str(u)
-        tt(un("s", u), xw(t).indirect(tab("NL", u)), un("z", u), ALU.add, XK + ["NL" + s, "z" + s], ["s" + s], W, 1, GAT)
-        act(un("z", u), un("s", u), ACT.Identity, 79.75, 0.5, ["s" + s], ["z" + s], W)
+        z, zk = zap(u, S - 1)
+        act(un("yg", u), xw(t).indirect(lst_(u, 0, 1)), ACT.Identity, 160.0, 1.0, keys + ["NL" + s], ["yg" + s], W, GAT)
+        ts(un("vb", u), reg(u, 3), 15.0 * LOW, None, ALU.add, None, ["pc" + s], ["vb" + s], W)
+        ts(tab("vT", u), last16("sc", u), col("ovT"), None, ALU.add, None, ["sc" + s, "covT"], ["vT" + s], WB)
+        tt(un("gt", u), un("yg", u), z, ALU.is_gt, ["yg" + s, zk], ["gt" + s], W)
+        mms([(reg(u, 4), T.BOb[:], un("gt", u), True, True)], ["BOb", "gt" + s], ["pc" + s], W)
+        own("sv", u, 4)
+        ts(tab("wt", u), last16("sv", u), col("ovo"), 2.0 ** -30, ALU.is_lt, ALU.add, ["sv" + s, "covo"], ["wt" + s], WB)
+        d = (u - rank) % NR
+        halve(un("zt", u), u, d, un("yg", u), "yg" + s, z, zk, "zt" + s)
+        if t == RO - 1:
+            act(un("vout", u), reg(u, 3), ACT.Identity, 15.0 * LOW + CEN, 1.0, ["pc" + s], ["vout" + s], W)
+        if d == 0:
+            c0 = B + W0N + K * t + W * rank
+            act(T.X[:, c0:c0 + W], un("zt", u), ACT.Identity, -160.0, 1.0, ["zt" + s], ["Xo%d" % t], W)
+        else:
+            k = u if u < rank else u - 1
+            act(T.snd[:, W * k:W * k + W], un("zt", u), ACT.Identity, -160.0, 1.0, ["zt" + s], ["snd%d" % k], W)
+        act(un("VX", u), un("yg", u), ACT.Identity, col("fb"), col("fs"), ["yg" + s, "cfb", "cfs"], ["VX" + s], W)
 
-    peers = [T.cores[q] for q in range(len(T.cores)) if q != rank]
-
-    def finish(t, u):
+    def after(t, u):
         s = str(u)
-        act(un("yg", u), xw(t).indirect(tab("NL", u)), ACT.Identity, 160.0, 1.0, XK + ["NL" + s], ["yg" + s], W, GAT)
-        mms([(pe(u), T.BOh[:], un("sA", u), True, True)], ["BOh", "sA" + s], ["pc" + s], W)
-        cp(un("vb", u), pe(u), ["pc" + s], ["vb" + s], W)
-        ts(tab("vT", u), last16("sc", u), float(-CEN - 1), None, ALU.add, None, ["sc" + s], ["vT" + s], WB)
-        ts(tab("vX", u), last16("sc", u), float(B + CEN), None, ALU.add, None, ["sc" + s], ["vX" + s], WB)
-        tt(un("gt", u), un("yg", u), un("z", u), ALU.is_gt, ["yg" + s, "z" + s], ["gt" + s], W, 2)
-        mms([(pc(u), T.IDh[:], T.MK0[:, 0:W], True, False)], ["IDh", "MK0"], ["pc" + s], W)
-        mms([(pc(u), T.BOb[:], un("gt", u), False, True)], ["BOb", "gt" + s], ["pc" + s], W)
-        scn(un("sv", u), pc(u), W, ["pc" + s], ["sv" + s])
-        ts(tab("wt", u), last16("sv", u), 9.0, 2.0 ** -9, ALU.is_lt, ALU.add, ["sv" + s], ["wt" + s], WB)
-        tt(un("s2", u), un("yg", u), un("z", u), ALU.add, ["yg" + s, "z" + s], ["s2" + s], W, 2)
-        act(un("z", u), un("s2", u), ACT.Identity, -0.25, 0.5, ["s2" + s], ["z" + s], W)
-        for b in range(W // 64):
-            q = W // 64 * u + b
-            d = (q - rank) % len(T.cores)
-            zz = T.z[:, 64 * q:64 * q + 64]
-            if d == 0:
-                c0 = B + W0N + K * t + 64 * rank
-                act(T.X[:, c0:c0 + 64], zz, ACT.Identity, -160.0, 1.0, ["z" + s], ["Xo%d" % t], 64)
-            else:
-                k = q if q < rank else q - 1
-                pp = T["pc" + s][:, 64 * b:64 * b + 64]
-                mms([(pp, T["PM%d" % d][:], zz, True, True)], ["PM%d" % d, "z" + s], ["pc" + s], 64)
-                act(T.snd[:, 64 * k:64 * k + 64], pp, ACT.Identity, -160.0, 1.0, ["pc" + s], ["snd%d" % k], 64)
+        prep(t, u)
+        mms([(reg(u, 5), T.IDh[:], un("AT", u), True, False), (reg(u, 5), T.IDh[:], un("NW%d" % t, u), False, True)],
+            ["IDh", "AT" + s, "NW%d" % t], ["pc" + s], W)
+        act(un("VA", u), reg(u, 5), ACT.Identity, col("va%d" % t), 1.0, ["pc" + s, "cva%d" % t], ["VA" + s], W)
+        c0 = B + W0N + K * t + W * u
+        ts(T.A[:, c0:c0 + W], un("AT", u), col("m15"), col("nw15"), ALU.mult, ALU.add, ["AT" + s, "cm15", "cnw15"], ["An%d%s" % (t, s)], W)
 
     def send(t):
         used = []
         trs = [None] * len(peers)
-        c0 = B + W0N + K * t + 64 * rank
+        c0 = B + W0N + K * t + W * rank
         for k in sorted(range(len(peers)), key=lambda k: topo.chip(peers[k]) == topo.chip(core)):
-            en = [e for e in topo.engines(core, peers[k]) if e not in used][:4]
+            en = [e for e in topo.engines(core, peers[k]) if e not in used][:ENG]
             used += en
             rid, pid = topo.addr(peers[k])[:2]
             trs[k] = RemoteDMATransfer(dst_ids=[DstId(rid=rid, pnc=pid)], dma_engine_mask=sum(1 << e for e in en),
-                                       remote_sem=T.sem["arr%d" % t], src=T.snd[:, 64 * k:64 * k + 64], dst=T.X[:, c0:c0 + 64])
+                                       remote_sem=T.sem["arr%d" % t], src=T.snd[:, W * k:W * k + W], dst=T.X[:, c0:c0 + W])
         rec("G", "send", lambda: g.remote_dma_fused(trs, local_sem=T.sem.snt), ["snd%d" % k for k in range(len(peers))],
             ["Xa%d" % t], 1.5, 4.0, "arr%d" % t)
 
-    def pairs(k, c0, c1):
-        u = k // WB
-        ts(T.EQ[:, 256 * k + c0:256 * k + c1], T.vb[:, c0:c1], T.vT[:, k:k + 1], T.wt[:, k:k + 1], ALU.is_equal, ALU.mult,
-           ["vb%d" % v for v in range(c0 // W, c1 // W)] + ["vT%d" % u, "wt%d" % u], ["EQ%d_%d" % (k, c0)], c1 - c0, 0.5)
+    half = NU // 2
+    mine = [u for u in range(NU) if u // half == rank // half]
+    ORD = [u for u in range(NU) if u not in mine] + [u for u in mine if u != rank] + [rank]
+    PX = "pd%d" % ORD[0]
 
-    def sums(ps, k, c0, c1, mats, last=False):
-        a, b = 16 * k, 16 * k + 16
-        lst = []
-        nn = 0
-        for lo, hi, m in ((c0, min(a, c1), "FBb"), (a, b, "MTb"), (max(b, c0), c1, "NBb")):
-            if lo < hi and lo >= c0 and hi <= c1 and m in mats:
-                lst.append((T[ps][:, lo:hi], T[m][:], T.EQ[:, 256 * k + lo:256 * k + hi], False, last))
-                nn += max(64, hi - lo)
-        if lst:
-            mms(lst, list(mats) + ["EQ%d_%d" % (k, c0)], [ps], nn / len(lst))
-
-    def joint(u):
-        s = str(u)
-        if u == 0:
-            mms([(T.pd0[:, 0:256], T.IDh[:], T.MKl[:], True, False), (T.pd0[:, 0:256], T.IDh[:], T.MK2[:], False, False)],
-                ["IDh", "MKl", "MK2"], ["pd0"], 256)
-        mms([(T.pd0[:, W * u:W * u + W], T.BOh[:], un("sA", u), False, False)], ["BOh", "sA" + s], ["pd0"], W)
-        for k in range(WB * u):
-            pairs(k, W * u, W * u + W)
-            sums("pd0", k, W * u, W * u + W, ("NBb",))
+    def pairs(t, u, c0, c1, last):
+        mats = ("FB", "MT", "NB") if t == RO - 1 else ("FS", "MS", "NB")
         for k in range(WB * u, WB * u + WB):
-            pairs(k, 0, W * u + W)
-            if u < NU - 1:
-                sums("pd0", k, 0, W * u + W, ("FBb", "MTb", "NBb"))
-            else:
-                sums("pd0", k, 0, K, ("MTb", "NBb"), k == 15)
+            e = "EQ%d_%d" % (k, c0)
+            ts(T.EQ[:, 256 * k + c0:256 * k + c1], T.vb[:, c0:c1], T.vT[:, k:k + 1], T.wt[:, k:k + 1], ALU.is_equal, ALU.mult,
+               ["vb%d" % v for v in range(c0 // W, c1 // W)] + ["vT%d" % u, "wt%d" % u], [e], c1 - c0, 0.5)
+            a, b = 16 * k, 16 * k + 16
+            lst = [(lo, hi, m) for (lo, hi), m in zip(((c0, min(a, c1)), (a, b), (max(b, c0), c1)), mats) if c0 <= lo < hi <= c1]
+            mms([(T[PX][:, lo:hi], T[m][:], T.EQ[:, 256 * k + lo:256 * k + hi], False, last and k == WB * u + WB - 1 and i == len(lst) - 1)
+                 for i, (lo, hi, m) in enumerate(lst)], [m for _, _, m in lst] + [e], [PX],
+                sum(max(64, hi - lo) for lo, hi, _ in lst) / len(lst))
 
-    def settle(t):
-        f = T.scL[:, 15:256:16]
-        scn(T.scL[:], T.pd0[:, 0:256], 256, ["pd0"], ["scL"])
-        if t < RO - 1:
-            tt(T.ofs[:], f, T.TR[:], ALU.max, ["scL", "TR"], ["ofs"], 16, 2)
-            cp(T.OFF[:], T.ofs[:], ["ofs"], ["OFF"], 16)
-            cp(aw(t).indirect(T.OFF[:]), T.VA[:], ["VA", "OFF"], AK, 256, 3.0)
-        stage[0] = 20 * t + 17.5
-        mms([(T.pd1[:, 0:256], T.IDh[:], T.MKl[:], True, False)], ["IDh", "MKl"], ["pd1"], 256)
-        for k in range(16 - WB, 16):
-            sums("pd1", k, 0, 256, ("FBb",), k == 15)
-        tt(T.fd[:], f, T.vX[:], ALU.subtract, ["scL"] + ["vX%d" % u for u in range(NU)], ["fd"], 16, 2)
-        scn(T.scM[:], T.pd1[:, 0:256], 256, ["pd1"], ["scM"])
-        tt(T.fe[:], T.fd[:], T.scM[:, 15:256:16], ALU.add, ["fd", "scM"], ["fe"], 16, 2)
-        ts(T.ff[:], T.fe[:], 0.0007, None, ALU.is_lt, None, ["fe"], ["ff"], 16)
-        tt(T.fm[:], T.ff[:], f, ALU.mult, ["ff", "scL"], ["fm"], 16, 2)
-        tt(T.fo[:], T.fm[:], T.TR[:], ALU.max, ["fm", "TR"], ["fo"], 16, 2)
-        cp(T.OFX[:], T.fo[:], ["fo"], ["OFX"], 16)
-        cp(xw(t).indirect(T.OFX[:]), T.VX[:], ["VX", "OFX"], XK, 256, 3.0)
+    def opened(c0, c1, start):
+        lst = [(T[PX][:, 0:K], T.IDh[:], T.MK0[:], True, False)] if start else []
+        mms(lst + [(T[PX][:, c0:c1], T.IDh[:], T.vb[:, c0:c1], False, False)],
+            ["IDh", "MK0"] + ["vb%d" % v for v in range(c0 // W, c1 // W)], [PX], 192 if start else c1 - c0)
 
-    def newlinks(t):
-        ts(T.AF[:], aw(t).indirect(T.NL[:]), col("nr%d" % t), None, ALU.mult, None,
-           AK + ["NL%d" % u for u in range(NU)] + ["cnr%d" % t], ["AF"], 256, 1, GAT)
-        tt(T.VA[:], T.AF[:], T["NW%d" % t][:], ALU.add, ["AF", "NW%d" % t], ["VA"], 256, 2)
-        c0 = B + W0N + K * t
-        ts(T.A[:, c0:c0 + K], T.AF[:], col("m15"), col("m15m"), ALU.mult, ALU.add, ["AF", "cm15", "cm15m"], ["An%d" % t], 256)
+    def joint(t, j):
+        def hf(u):
+            return (K // 2 * (u // half), K // 2 * (u // half) + K // 2)
 
+        def one(u):
+            return (W * u, W * u + W)
+        h0, h1 = hf(ORD[0]), hf(ORD[-1])
+        if j == 0:
+            return
+        if j == 1:
+            opened(h0[0], h0[1], True)
+            todo = [(ORD[0], h0), (ORD[1], h0)]
+        elif not FINE:
+            if j == 3:
+                opened(h1[0], h1[1], False)
+            todo = [(ORD[2], h0)] if j == 2 else [(ORD[0], h1), (ORD[1], h1), (ORD[2], h1), (ORD[3], (0, K))]
+        else:
+            opened(W * ORD[j], W * ORD[j] + W, False)
+            todo = [(u, one(ORD[j])) for u in ORD[:j]]
+            todo += [(ORD[2], h0), (ORD[2], one(ORD[2]))] if j == 2 else [(ORD[3], (0, K))]
+        for i, (u, c) in enumerate(todo):
+            pairs(t, u, c[0], c[1], j == 3 and i == len(todo) - 1)
+
+    def places(off):
+        op("V", lambda: g.vector.tensor_tensor_scan(T.scX[:], T.D0[:], T[PX][:, 0:K], 1e9, ALU.min, ALU.max), ["D0", PX], ["scX"], vd(K))
+        ts(T[off][:], T.scX[:, 15:K:16], CEN + B - LIFT + 0.3, None, ALU.add, None, ["scX"], [off], 16)
+
+    old = XK
     for t in range(RO):
-        for u in range(NU):
-            stage[0] = 20 * t + 1 + u
-            s = str(u)
-            act(un("z", u), xw(max(t - 1, 0)).indirect(tab("NL", u)), ACT.Identity, 160.0, 1.0, XK + ["NL" + s], ["z" + s], W, GAT)
-            prep(t, u)
-        if t:
-            XK = XK + ["Xa%d" % (t - 1), "Xo%d" % (t - 1)]
+        if t == 0:
+            for j, u in enumerate(ORD):
+                stage[0] = 1 + j
+                prep(t, u)
+        else:
+            old, XK = XK, XK + ["Xa%d" % (t - 1), "Xo%d" % (t - 1)]
         for st in range(S):
-            for u in range(NU):
-                stage[0] = 20 * t + 1 + NU * st + u
-                bulk(t, u, st)
+            for j, u in enumerate(ORD):
+                stage[0] = 20 * t + 1 + NU * st + j
+                bulk(t, u, st, old, XK)
                 choose(t, u, st)
                 if st < S - 1:
                     prep(t, u)
-                    advance(t, u)
                 else:
-                    finish(t, u)
+                    finish(t, u, XK)
+                    if j == NU - 2:
+                        send(t)
                     stage[0] = 20 * t + 16.5
-                    joint(u)
-        stage[0] = 20 * t + 17
-        send(t)
-        act(T.VX[:], T.yg[:], ACT.Identity, col("fb"), col("fs"), ["yg%d" % u for u in range(NU)] + ["cfb", "cfs"], ["VX"], 256)
-        if t < RO - 1:
-            newlinks(t)
+                    joint(t, j)
+                    if t < RO - 1:
+                        stage[0] = 20 * t + 16.7
+                        after(t, u)
+            if t == RO - 1 and st == 0:
+                dma("Y", T.yx[1:128:2, 0:AC - B], T.X[1:128:2, B:AC], "dE", XK, [], 5.0)
+        stage[0] = 20 * t + 16.6
+        if t == RO - 1:
+            places("OFX")
         else:
-            ts(T.vout[:], T.vb[:], float(CEN), None, ALU.add, None, ["vb%d" % u for u in range(NU)], ["vout"], 256)
-            dma("Y", T.yv[:], T.vout[0:128:16, :], "dO", ["vout"], [], 2.0)
-        settle(t)
+            ts(T.vX[:], T.vT[:], float(LIFT), None, ALU.add, None, ["vT%d" % u for u in range(NU)], ["vX"], 16)
+            places("OFA")
+            tt(T.fe[:], T.scX[:, 15:K:16], T.vX[:], ALU.is_equal, ["scX", "vX"], ["fe"], 16)
+            tt(T.fm[:], T.fe[:], T.vX[:], ALU.mult, ["fe", "vX"], ["fm"], 16)
+            tt(T.fo[:], T.fm[:], T.D0[:, 0:K:16], ALU.max, ["fm", "D0"], ["fo"], 16)
+            ts(T.OFX[:], T.fo[:], float(CEN + B - LIFT), None, ALU.add, None, ["fo"], ["OFX"], 16)
+        cp(xw(t).indirect(T.OFX[:]), T.VX[:], ["VX%d" % u for u in range(NU)] + ["OFX"], XK, K, SCA)
         if t < RO - 1:
-            AK = AK + ["An%d" % t]
-    XK = XK + ["Xa%d" % (RO - 1), "Xo%d" % (RO - 1)]
-    dma("Y", T.yx[:], T.X[:, B:B + W0N + RO * K], "dO", XK, [], 5.0)
+            stage[0] = 20 * t + 17
+            cp(aw(t).indirect(T.OFA[:]), T.VA[:], ["VA%d" % u for u in range(NU)] + ["OFA"], AK, K, SCA)
+            AK = AK + ["An%d%d" % (t, u) for u in range(NU)]
+    dma("Y", T.yx[0:128:2, 0:AC - B], T.X[0:128:2, B:AC], "dO", XK, [], 4.0)
+    dma("Y", T.yx[:, AC - B:XC - B], T.X[:, AC:XC], "dO", ["Xa%d" % (RO - 1), "Xo%d" % (RO - 1)], [], 2.0)
+    dma("Y", T.yv[:], T.vout[0:128:16, :], "dO", ["vout%d" % u for u in range(NU)], [], 2.0)
 
     n = len(recs)
     preds = [set() for _ in range(n)]
@@ -543,9 +618,9 @@ def rank_program(g, core, T, topo):
             who = q + sem
         else:
             fn()
-            cnt["snt"] = cnt.get("snt", 0) + 4 * len(peers)
+            cnt["snt"] = cnt.get("snt", 0) + ENG * len(peers)
             rtok = ("snt", cnt["snt"], dict(known[q]))
-            cnt[sem] = 4 * len(peers)
+            cnt[sem] = ENG * len(peers)
             tok = (sem, cnt[sem], {})
             who = "rem"
         for k in writes:

@@ -9,24 +9,32 @@ W0N, K, RO, S = 3072, 256, 3, 4
 NU = 4
 W = K // NU
 WB = W // 16
-B = 272
+B = 384
 CEN = 1919
 LOW = 2048
-LIFT = 4096
 HOLD = 8192
-PG = 4
-CUT = (1, 8)
+BIG = 2.0 ** 23
+PG = 2
+XG = 2
 ZQ = "V"
-FINE = True
+ZP = True
+HELP = 32
+PAIRS = {1: [(0, 0, 2), (1, 0, 2)], 2: [(2, 0, 3)], 3: [(0, 2, 4), (1, 2, 4), (2, 3, 4), (3, 0, 3), (3, 3, 4)]}
 XC = B + W0N + RO * K
 AC = B + W0N + (RO - 1) * K
 CYC = 0.00083
 PEC = 0.00042
-GAT = 1.45
+GAT = 1.56
+NLATE = 2
+GV = 3
 SCA = 3.8
 WK = 0.26
-LOOK = 0.02
-LATE = 12
+TURNS = 3
+SOFT = 1
+AFTER = True
+SPLIT = False
+LOOK = {"V": 0.02, "S": 0.02, "P": 0.02, "G": 0.02, "Y": 0.02}
+LATE = 0.5
 ENG = 4
 
 SCRATCH = {}
@@ -39,37 +47,37 @@ def _b(name, cols, dtype, where="sbuf"):
 _b("X", XC, "bfloat16")
 _b("A", AC, "int32")
 _b("WL", 16, "int32")
-for _n in ("OFA", "OFX"):
+for _n in ("NL", "LL", "OFA", "OFX"):
     _b(_n, 16, "uint16")
-for _n in ("z", "zt", "ok", "gt", "yg", "VX", "cT", "J", "JM", "ta", "tb", "tc", "td", "te", "tf"):
+for _n in ("z", "zr", "zt", "s", "xl", "ok", "gt", "yg", "VX", "J", "J2", "JM", "PH", "ta", "tb", "tc", "te", "tf"):
     _b(_n, 256, "bfloat16")
-for _n in ("AT", "T1", "sA0", "sA1", "sA2", "sA3", "vb", "MK0", "NW0", "NW1"):
+for _n in ("AT", "sA0", "sA1", "sA2", "sA3", "vb", "MK0", "NW0", "NW1"):
     _b(_n, 256, "float16")
 _b("LT", 256, "uint16")
-_b("xg0", 16 * 256, "bfloat16")
-_b("xg1", 16 * 256, "bfloat16")
-_b("mn", 16 * 256, "bfloat16")
+_b("xg", 16 * 256, "bfloat16")
+_b("mn", 15 * 256, "bfloat16")
 for _u in range(NU):
     _b("pd%d" % _u, 512, "float32", "psum")
     _b("pc%d" % _u, 512, "float32", "psum")
-for _n in ("vT", "wt", "vX", "fe", "fm", "fo"):
-    _b(_n, 16, "float32")
 _b("EQ", 16 * 256, "bfloat16")
-for _n in ("sc", "sv", "scX", "VA", "vout", "JC", "D0"):
+for _n in ("sc", "sv", "scX", "scA", "VA", "vout", "JC", "D0"):
     _b(_n, 256, "float32")
-_b("M", W, "float32")
+for _n in ("M", "D1", "D2", "JB"):
+    _b(_n, W, "float32")
+_b("MKs", W, "float16")
+_b("MKv", W, "bfloat16")
 _b("snd", 192, "bfloat16")
 _b("PI", 8, "int32")
 _b("PJ", 16, "float32")
 _b("col", 64, "float32")
-_b("W1", 248, "bfloat16")
-_b("W2", 248, "bfloat16")
-for _n in ("JG", "JE", "J8", "BOb", "NB", "FB", "MT", "FS", "MS", "ZS", "TRI0", "TRI1", "TRI2", "PH0", "PH1", "PH2", "PH3"):
+_b("W1", 144, "bfloat16")
+_b("W2", 144, "bfloat16")
+for _n in ("JG", "JP", "BOb", "BOn", "NB", "FB", "MT", "MU", "MA", "ZS", "IDb", "TRI0", "TRI1", "TRI2"):
     _b(_n, 128, "bfloat16")
-for _n in ("BOh", "IDh", "PAT", "DEAD", "SW00", "SW01", "SW10", "SW11", "RW0", "RW1"):
+for _n in ("BOh", "IDh", "DEAD", "RW0", "RW1"):
     _b(_n, 128, "float16")
 
-SEMAPHORES = ["qV", "qS", "qP", "qG", "dX", "dW", "dA", "dO", "dE", "arr0", "arr1", "arr2", "snt"]
+SEMAPHORES = ["qV", "qS", "qP", "qG", "dX", "dW", "dA", "dO", "dE", "arr0", "arr1", "arr2", "snt0", "snt1"]
 
 
 def rank_program(g, core, T, topo):
@@ -104,6 +112,9 @@ def rank_program(g, core, T, topo):
 
     def cp(out, in_, reads, writes, n, ind=None):
         op("V", lambda: g.vector.tensor_copy(out, in_), reads, writes, vd(n, 1.0, ind))
+
+    def scan(out, d0, d1, init, op0, op1, reads, writes, n):
+        op("V", lambda: g.vector.tensor_tensor_scan(out, d0, d1, init, op0, op1), reads, writes, vd(n))
 
     def act(out, in_, f, bias, scale, reads, writes, n=128, ind=1.0):
         op("S", lambda: g.scalar.activation(out, in_, f, bias=bias, scale=scale), reads, writes, 0.065 + n * CYC * ind)
@@ -150,107 +161,93 @@ def rank_program(g, core, T, topo):
     def ck(name):
         return "PJ" if name[0] == "P" else "c" + name
 
+    def sc_(s):
+        return col(s) if isinstance(s, str) else s
+
     def mkcol(name, src, s1, s2, op0, op1):
         in0, key = (T.PI[:, src:src + 1], "PI%d" % src) if isinstance(src, int) else (col(src), ck(src))
-        rd = [key] + [ck(s) for s in (s1, s2) if isinstance(s, str)]
-        ts(newcol(name), in0, col(s1) if isinstance(s1, str) else s1, col(s2) if isinstance(s2, str) else s2, op0, op1, rd, ["c" + name], 1)
+        ts(newcol(name), in0, sc_(s1), sc_(s2), op0, op1, [key] + [ck(s) for s in (s1, s2) if isinstance(s, str)], ["c" + name], 1)
 
-    def mat(out, src, s1, s2, op0, op1, n=128):
-        rd = [src] + [ck(s) for s in (s1, s2) if isinstance(s, str)]
-        ts(T[out][:, 0:n], T[src][:, 0:n], col(s1) if isinstance(s1, str) else s1, col(s2) if isinstance(s2, str) else s2,
-           op0, op1, rd, [out], n, 0.5)
+    def mat(out, src, s1, s2, op0, op1, n=128, f=0.5):
+        ts(T[out][:, 0:n], T[src][:, 0:n], sc_(s1), sc_(s2), op0, op1, [src] + [ck(s) for s in (s1, s2) if isinstance(s, str)], [out], n, f)
 
     def mat2(out, a, b, o, n=128, f=1.0):
         tt(T[out][:, 0:n], T[a][:, 0:n], T[b][:, 0:n], o, [a, b], [out], n, f)
 
-    def lst_(u, a, b):
-        return T.LT[:, 16 * WB * u + WB * a:16 * WB * u + WB * b]
-
     iota(T.PI[:, 0:1], "PI0", [[0, 1]], 0, 1, 1, True)
     iota(T.PJ[:], "PJ", [[16, 16]], -112, 1, 16)
-    iota(T.J[:], "J", [[1, 256]], 0, 0, 256)
-    iota(T.J8[:], "J8", [[0, 16], [16, 8]], 0, 0, 128)
-    iota(T.JE[:], "JE", [[1, 2], [2, 8], [0, 8]], 0, 0, 128)
     iota(T.JG[:], "JG", [[16, 8], [0, 16]], 0, 0, 128)
     iota(T.JM[:], "JM", [[0, 16], [1, 16]], 0, 0, 256)
+    iota(T.J[:], "J", [[1, 256]], 0, 0, 256)
     op("V", lambda: g.vector.memset(T.A[:, 0:B], -1), [], ["Am"], vd(B))
     op("V", lambda: g.vector.memset(T.X[:, 0:B], 95.0), [], ["Xm"], vd(B, 0.5))
-    for i, m in ((1, 15), (2, 16), (3, 1), (4, 7), (5, 56), (6, 64)):
+    for i, m in ((1, 15), (3, 1)):
         ts(T.PI[:, i:i + 1], T.PI[:, 0:1], m, None, ALU.bitwise_and, None, ["PI0"], ["PI%d" % i], 1)
     mkcol("R", 1, 0.0, None, ALU.add, None)
-    mkcol("U1", 2, 0.0625, None, ALU.mult, None)
-    mkcol("U0", 2, -0.0625, 1.0, ALU.mult, ALU.add)
     mkcol("G", "R", -1.0, "P0", ALU.mult, ALU.add)
+    mkcol("G15", "G", 15.0, None, ALU.add, None)
     mkcol("m15", "R", 15.0, None, ALU.is_equal, None)
-    mkcol("g8", 4, 16.0, None, ALU.mult, None)
-    mkcol("e2", 5, 0.25, None, ALU.mult, None)
-    mkcol("E", 6, 1.0 / 64, "e2", ALU.mult, ALU.add)
-    mkcol("e0", "E", 0.0, 1e9, ALU.is_equal, ALU.mult)
-    mkcol("thr0", "e0", 68.0, None, ALU.add, None)
+    mkcol("RP", "m15", -16.0, "R", ALU.mult, ALU.add)
     for k in range(1, S):
-        mkcol("thr%d" % k, "E", -float(LOW * k), "thr0", ALU.mult, ALU.add)
-    mkcol("R1", "R", 1.0, None, ALU.add, None)
-    mkcol("RE", "m15", -16.0, "R1", ALU.mult, ALU.add)
+        mkcol("thr%d" % k, "RP", -float(LOW * k), 68.0 - LOW * k, ALU.mult, ALU.add)
     mkcol("r0", "R", 0.0, 2.0 * HOLD, ALU.is_equal, ALU.mult)
     mkcol("oNL", "r0", float(CEN + B + 15 * LOW - HOLD), None, ALU.add, None)
     mkcol("Rb", "r0", 8.0 / HOLD, -1.0, ALU.mult, ALU.add)
     mkcol("Rm", "Rb", "R", None, ALU.add, None)
-    mkcol("e1", "E", 0.0, None, ALU.is_gt, None)
-    for u, h, n_ in ((0, 0, "P0"), (1, 1, "P0"), (0, 1, "P16"), (1, 0, "P-16")):
-        mat("SW%d%d" % (u, h), "J", n_, "U%d" % u, ALU.is_equal, ALU.mult)
-    for u in range(NU):
-        ts(lst_(u, 0, 1), T.WL[:, WB * u:WB * u + WB], float(B), None, ALU.add, None, ["WL"], ["NL%d" % u], WB)
-    mat("ZS", "J8", "G", None, ALU.is_equal, None)
-    mkcol("g120", "G", 0.0625, 120.0, ALU.mult, ALU.add)
-    mat("W1", "J", "g120", None, ALU.is_equal, None, 248)
-    mat("W2", "J", "g120", -2.0, ALU.is_equal, ALU.mult, 248)
-    mat("ta", "JE", "RE", None, ALU.is_equal, None)
-    mat2("PAT", "ta", "ZS", ALU.mult)
-    mat("td", "J8", "g8", None, ALU.is_equal, None)
-    mat("ta", "JE", "E", -2.0 * LOW, ALU.is_lt, ALU.mult)
-    mat("tb", "JE", "E", 2.0 * LOW, ALU.is_equal, ALU.mult)
+    ts(T.NL[:], T.WL[:], float(B), None, ALU.add, None, ["WL"], ["NL%d" % u for u in range(NU)], 16)
+    mat("BOb", "JG", "G", None, ALU.is_equal, None)
+    mat("ta", "JM", 15.0, None, ALU.is_lt, None)
+    mat2("ZS", "ta", "BOb", ALU.mult)
+    mat("W1", "J", "G15", None, ALU.is_equal, None, 144)
+    mat("W2", "J", "G15", -2.0, ALU.is_equal, ALU.mult, 144)
+    mat("IDb", "J", "P0", None, ALU.is_equal, None)
+    mat("IDh", "J", "P0", None, ALU.is_equal, None)
+    mat("tb", "JM", 15.0, -16.0, ALU.is_equal, ALU.mult)
+    mat2("JP", "tb", "JM", ALU.add)
+    mat("ta", "JP", "RP", -2.0 * LOW, ALU.is_lt, ALU.mult)
+    mat("tb", "JP", "RP", 2.0 * LOW, ALU.is_equal, ALU.mult)
     mat2("tc", "ta", "tb", ALU.add)
-    mat2("te", "tc", "td", ALU.mult)
+    mat2("te", "tc", "BOb", ALU.mult)
     for t in range(RO):
         stage[0] = LATE if t else 0
-        mkcol("rv%d" % t, "E", float(14 + t), None, ALU.is_lt, None)
-        mat("tf", "JE", float(14 + t), "rv%d" % t, ALU.is_lt, ALU.mult)
+        mkcol("rv%d" % t, "RP", float(13 + t), None, ALU.is_lt, None)
+        mat("tf", "JP", float(13 + t), "rv%d" % t, ALU.is_lt, ALU.mult)
         mat2("TRI%d" % t, "tf", "te", ALU.mult)
     stage[0] = 0
-    mat("BOh", "JG", "g8", None, ALU.is_equal, None)
+    mat("BOh", "JG", "G", None, ALU.is_equal, None)
     mat("ta", "JM", "R", float(HOLD), ALU.is_equal, ALU.mult, W)
     mat("tb", "JM", "Rm", -2.0 * HOLD, ALU.is_equal, ALU.mult, W)
     mat2("M", "ta", "tb", ALU.add, W, 2)
-    mat("tc", "JE", "E", "e1", ALU.is_ge, ALU.mult)
-    mat2("DEAD", "tc", "td", ALU.mult)
-    HALF = 127.0 / 256
-    mat("PH0", "J", "P0", HALF, ALU.is_equal, ALU.mult)
+    mat("tc", "JM", "R", None, ALU.is_ge, None)
+    mat2("DEAD", "tc", "ZS", ALU.mult)
     stage[0] = LATE
-    iota(T.JC[:], "JC", [[-16, 16], [0, 16]], 240 - CEN - B + LIFT, 0, 256)
+    HALF = 127.0 / 256
+    iota(T.J2[:], "J2", [[0, 2], [1, 128]], 0, 0, 256)
+    iota(T.JC[:], "JC", [[-16, 16], [0, 16]], 240 - CEN - B, 1, 256)
+    iota(T.JB[:], "JB", [[0, W]], int(BIG), 0, W)
+
+    def starts(out, src, n, keep, fill):
+        op("G", lambda: g.affine_select(T[out][:], T[src][:], [[0, n // 16], [1, 16]], keep, fill, 0, 0), [src], [out], 0.17 + 2 * CYC * n)
+    starts("D0", "JC", K, ALU.is_equal, BIG)
+    starts("D1", "JB", W, ALU.not_equal, -2.0 * LOW)
+    starts("D2", "JB", W, ALU.not_equal, 2.0 ** -30)
     mkcol("fs", 3, 2.0, -1.0, ALU.mult, ALU.add)
     mkcol("fb", 3, -335.0, 175.0, ALU.mult, ALU.add)
     mkcol("nw15", "m15", CEN + 1.0, -1.0, ALU.mult, ALU.add)
-    mkcol("ovT", "r0", float(15 * LOW - HOLD), None, ALU.add, None)
     mkcol("oLL", "r0", float(CEN + B - HOLD), None, ALU.add, None)
-    mkcol("ovo", "r0", -1.0, 9.0 + HOLD, ALU.mult, ALU.add)
-    mat("BOb", "JG", "G", None, ALU.is_equal, None)
-    mat("IDh", "J", "P0", None, ALU.is_equal, None)
-    for d in range(1, NR):
-        mat("ta", "J", "P%d" % (16 * d), HALF, ALU.is_equal, ALU.mult)
-        mat("tb", "J", "P%d" % (16 * d - 128), HALF, ALU.is_equal, ALU.mult)
-        mat2("PH%d" % d, "ta", "tb", ALU.add)
-    mat("ta", "JM", "R", 2.0 * LIFT, ALU.is_equal, ALU.mult, 256)
-    mat("MK0", "ta", -float(LIFT), None, ALU.add, None, 256)
+    mat("PH", "J2", "P0", HALF, ALU.is_equal, ALU.mult, 256)
+    mat("MK0", "JM", "R", -float(HOLD), ALU.not_equal, ALU.mult, 256)
+    mat("MKs", "MK0", 15.0 * LOW, None, ALU.add, None, W)
+    mat("MKv", "MK0", 8.5, None, ALU.add, None, W)
+    mat("BOn", "JG", "G", -1.0, ALU.is_equal, ALU.mult)
     mat("NB", "JG", "G", -2.0 ** 43, ALU.is_equal, ALU.mult)
-    mat("FB", "JG", "G", -2.0 ** 13, ALU.is_equal, ALU.mult)
-    mat("FS", "JG", "G", -2.0 ** -10, ALU.is_equal, ALU.mult)
+    mat("FB", "JG", "G", -2.0 ** 14, ALU.is_equal, ALU.mult)
     mat("ta", "JM", "R", None, ALU.is_gt, None)
-    mat2("tb", "ta", "NB", ALU.mult)
-    mat2("MT", "tb", "FB", ALU.min)
-    mat2("MS", "tb", "FS", ALU.min)
-    mat("ta", "JM", 0.0, 2.0 ** 30, ALU.is_gt, ALU.mult, 256)
-    ts(T.JC[:], T.JC[:], col("R"), None, ALU.add, None, ["JC", "cR"], ["JC"], 256)
-    mat2("D0", "ta", "JC", ALU.add, 256, 2)
+    mat2("MA", "ta", "NB", ALU.mult)
+    mat2("MT", "MA", "FB", ALU.min)
+    mat("tb", "JM", "R", None, ALU.is_ge, None)
+    mat2("tc", "tb", "NB", ALU.mult)
+    mat2("MU", "tc", "FB", ALU.min)
     for t in range(RO - 1):
         mkcol("rt%d" % t, "R", float(13 + t), None, ALU.is_equal, None)
         mkcol("va%d" % t, "rt%d" % t, 2048.0, float(CEN), ALU.mult, ALU.add)
@@ -258,19 +255,19 @@ def rank_program(g, core, T, topo):
         mat("RW%d" % t, "JG", "G", "rt%d" % t, ALU.is_equal, ALU.mult)
 
     def un(name, u):
+        if name in ("vb", "sc", "sv", "VX", "VA"):
+            u = ORD.index(u)
         return T[name][:, W * u:W * u + W]
 
     def tab(name, u):
         return T[name][:, WB * u:WB * u + WB]
 
     def last16(name, u):
+        u = ORD.index(u)
         return T[name][:, W * u + 15:W * u + W:16]
 
     def reg(u, k):
         return T["pc%d" % u][:, W * k:W * k + W]
-
-    def xgp(step, u, a, b):
-        return T["xg%d" % (step % 2)][:, 16 * W * u + W * a:16 * W * u + W * b]
 
     def xw(t):
         return T.X[:, 0:B + W0N + K * t]
@@ -279,117 +276,111 @@ def rank_program(g, core, T, topo):
         return T.A[:, 0:B + W0N + K * t]
 
     def own(out, u, k):
-        s = str(u)
-        op("V", lambda: g.vector.tensor_tensor_scan(un(out, u), reg(u, k), T.M[:], -1e6, ALU.max, ALU.add), ["M", "pc" + s], [out + s], vd(W))
-
-    def links(t, u):
-        s = str(u)
-        ts(un("AT", u), aw(t).indirect(lst_(u, 0, 1)), float(-CEN), None, ALU.add, None, AK + ["NL" + s], ["AT" + s], W, 1, GAT)
+        scan(un(out, u), reg(u, k), T.M[:], -1e6, ALU.max, ALU.add, ["M", "pc%d" % u], [out + str(u)], W)
 
     def prep(t, u):
         s = str(u)
-        links(t, u)
-        nb = W // 32
-        o = W * u
-        for b in range(nb):
-            op("V", lambda b=b: g.vector.transpose(T.T1[:, o + b:o + W:nb], T.AT[:, o + 32 * b:o + 32 * b + 32]),
-               ["AT" + s], ["T1%s%d" % (s, b)], vd(32))
-        lst = []
-        for v in range(2):
-            for h in range(2):
-                lst.append((T["pc" + s][:, W + v:2 * W:2], T["SW%d%d" % (v, h)][:],
-                            T.T1[:, o + W // 2 * h:o + W // 2 * h + W // 2], h == 0, h == 1))
-        mms(lst, ["T1%s%d" % (s, b) for b in range(nb)] + ["SW00", "SW01", "SW10", "SW11"], ["pc" + s], W // 2)
-        n = WB * (13 + t)
-        ts(lst_(u, 1, 14 + t), T["pc" + s][:, W:W + n], float(CEN + B), None, ALU.add, None, ["pc" + s], ["LT" + s], n)
+        ts(un("LT", u), aw(t).indirect(tab("NL", u)), float(B), None, ALU.add, None, AK + ["NL" + s], ["LT" + s], W, 1, GAT)
+        ts(un("AT", u), un("LT", u), -float(B + CEN), None, ALU.add, None, ["LT" + s], ["AT" + s], W, 0.5)
 
     def newlist(t, u):
         s = str(u)
-        links(t, u)
-        mms([(reg(u, 6), T["RW%d" % t][:], un("AT", u), True, True)], ["RW%d" % t, "AT" + s], ["pc" + s], W)
-        own("sv", u, 6)
-        ts(lst_(u, 14 + t, 15 + t), last16("sv", u), col("oLL"), None, ALU.add, None, ["sv" + s, "coLL"], ["LL" + s], WB)
+        ts(un("AT", u), aw(t).indirect(tab("NL", u)), -float(CEN), None, ALU.add, None, AK + ["NL" + s], ["AT" + s], W, 1, GAT)
+        ps = "pd%d" % ORD[-1]
+        mms([(T[ps][:, 0:W], T["RW%d" % t][:], un("AT", u), True, True)], ["RW%d" % t, "AT" + s], [ps], W)
+        scan(un("sv", u), T[ps][:, 0:W], T.M[:], -1e6, ALU.max, ALU.add, ["M", ps], ["sv" + s], W)
+        ts(tab("LL", u), last16("sv", u), col("oLL"), None, ALU.add, None, ["sv" + s, "coLL"], ["LL" + s], WB)
 
-    def halve(out, u, d, y, ykey, z, zkey, okey):
+    def advance(t, u, step, keys, j):
         s = str(u)
-        mms([(reg(u, 0), T["PH%d" % d][:], z, True, False), (reg(u, 0), T["PH%d" % d][:], y, False, True)],
-            ["PH%d" % d, ykey, zkey], ["pc" + s], W)
-        if ZQ == "V" and okey[0:2] != "zt":
-            ts(out, reg(u, 0), 1.0, None, ALU.add, None, ["pc" + s], [okey], W)
+        if step == 0:
+            ts(un("z", u), xw(max(t - 1, 0)).indirect(tab("NL", u)), 160.0, None, ALU.add, None, keys + ["NL" + s], ["z" + s], W, 1, GAT)
         else:
-            act(out, reg(u, 0), ACT.Identity, 1.0, 1.0, ["pc" + s], [okey], W)
+            tt(un("s", u), xw(t).indirect(tab("NL", u)), un("z", u), ALU.add, keys + ["NL" + s, "z" + s], ["s" + s], W, 1, GAT)
+            if ZQ == "V":
+                ts(un("z", u), un("s", u), 0.5, 79.75, ALU.mult, ALU.add, ["s" + s], ["z" + s], W, 0.5)
+            else:
+                act(un("z", u), un("s", u), ACT.Identity, 79.75, 0.5, ["s" + s], ["z" + s], W)
+        if ZP:
+            mms([(reg(u, 7), T.IDb[:], un("z", u), True, True)], ["IDb", "z" + s], ["pc" + s], W)
+        if step == S - 1 and j >= GV:
+            act(un("zr", u), un("z", u), ACT.Identity, -160.0, 1.0, ["z" + s], ["zr" + s], W)
 
-    def zap(u, step):
-        return (xgp(0, u, 0, 1), "xw0%d_0" % u) if step == 0 else (un("z", u), "z%d" % u)
-
-    def bulk(t, u, step, old, new):
+    def bulk(t, u, step, j, old, new):
         s = str(u)
         nl = 13 + t
-        p = step % 2
-        late = step == 0 and t > 0
-        cuts = [0] + list(CUT) + ([nl] if late else []) + [nl + 1]
+        late = step == 0 and t > 0 and j < NLATE
         pd = T["pd" + s][:, 0:W]
+        o = 16 * W * u
+        win, keys = (xw(t - 1), old) if late else (xw(t), new)
+        if step == 0:
+            if t and not late:
+                prep(t - 1, u)
+            advance(t, u, step, old, j)
+        n = HELP if step == 0 and j == 0 and t == 0 else 0
+        if n:
+            ts(T.xg[:, o:o + 16 * n], win.indirect(T.LT[:, W * u:W * u + n]), 160.0, None, ALU.add, None, keys + ["LT" + s], ["xh" + s],
+               16 * n, 1, GAT)
+        act(T.xg[:, o + 16 * n:o + 16 * W], win.indirect(T.LT[:, W * u + n:W * u + W]), ACT.Identity, 160.0, 1.0,
+            keys + ["LT" + s] + (["~L"] if j > 1 else []),
+            ["xg" + s] + ([] if n else ["xh" + s]), 16 * (W - n), GAT)
+        mms([(pd, T.DEAD[:], un("sA%d" % k, u), k == 0, False) for k in range(step)] + [(pd, T.ZS[:], un("z", u), step == 0, False)],
+            ["ZS", "z" + s, "DEAD"] + ["sA%d%s" % (k, s) for k in range(step)], ["pd" + s], W)
+        if late:
+            newlist(t - 1, u)
+        z, zk = (reg(u, 7), "pc" + s) if ZP else (un("z", u), "z" + s)
 
-        def mn(a, b):
-            return T.mn[:, W * (16 * u + a):W * (16 * u + b)]
-        for a, b in zip(cuts, cuts[1:]):
-            isnew = late and a == nl
-            if isnew:
-                newlist(t - 1, u)
-            win, keys = (xw(t - 1), old) if late and not isnew else (xw(t), new)
-            act(xgp(step, u, a, b), win.indirect(lst_(u, a, b)), ACT.Identity, 160.0, 1.0,
-                keys + (["LL" + s] if isnew else ["NL" + s] if b == 1 else ["NL" + s, "LT" + s]), ["xw%d%s_%d" % (p, s, i) for i in range(a, b)], W * (b - a), GAT)
-            if a == 0:
-                if step:
-                    z0, k0 = zap(u, step - 1)
-                    halve(un("z", u), u, 0, xgp(step, u, 0, 1), "xw%d%s_0" % (p, s), z0, k0, "z" + s)
-                z, zk = zap(u, step)
-            for i in range(max(a, 1), b):
-                tt(mn(i, i + 1), xgp(step, u, i, i + 1), z, ALU.min, [zk, "xw%d%s_%d" % (p, s, i)], ["mn%s_%d" % (s, i)], W)
-            if a == 0:
-                mms([(pd, T.DEAD[:], un("sA%d" % k, u), k == 0, False) for k in range(step)] + [(pd, T.ZS[:], z, step == 0, False)],
-                    ["ZS", zk, "DEAD"] + ["sA%d%s" % (k, s) for k in range(step)], ["pd" + s], W)
-            a = max(a, 1)
-            if a < b:
-                mms([(pd, row("W1", i), xgp(step, u, i, i + 1), False, False) for i in range(a, b)],
-                    ["W1"] + ["xw%d%s_%d" % (p, s, i) for i in range(a, b)], ["pd" + s], W)
-            while a < b:
-                d = min(b, a + (PG if a + PG <= nl - 1 else 2 if a + 2 <= nl else 1))
-                mms([(pd, row("W2", i), mn(i, i + 1), False, i == nl) for i in range(a, d)],
-                    ["W2"] + ["mn%s_%d" % (s, i) for i in range(a, d)], ["pd" + s], W)
-                a = d
-
-    def row(name, e):
-        o = 120 - 64 * (e % 2) - 8 * (e // 2)
-        return T[name][:, o:o + 128]
+        def part(a, b, x, xk):
+            for c in range(a, b, XG):
+                mms([(pd, T.W1[:, 15 - i:143 - i], x(i), False, False) for i in range(c, min(b, c + XG))], ["W1"] + xk, ["pd" + s], W)
+            for c in range(a, b, PG):
+                d = min(b, c + PG)
+                for i in range(c, d):
+                    tt(T.mn[:, W * (15 * u + i):W * (15 * u + i + 1)], x(i), z, ALU.min, [zk] + xk, ["mn%s_%d" % (s, i)], W)
+                mms([(pd, T.W2[:, 15 - i:143 - i], T.mn[:, W * (15 * u + i):W * (15 * u + i + 1)], False, i == nl - 1) for i in range(c, d)],
+                    ["W2"] + ["mn%s_%d" % (s, i) for i in range(c, d)], ["pd" + s], W)
+        part(0, nl - late, lambda i: T.xg[:, o + i:o + 16 * W:16], ["xg" + s, "xh" + s])
+        if late:
+            act(un("xl", u), xw(t).indirect(tab("LL", u)), ACT.Identity, 160.0, 1.0, new + ["LL" + s], ["xl" + s] + (["~L"] if j < SOFT else []), W, GAT)
+            part(nl - 1, nl, lambda i: un("xl", u), ["xl" + s])
 
     def choose(t, u, step):
         s = str(u)
         k = "sA%d" % step
-        ts(un("ok", u), T["pd" + s][:, 0:W], col("thr%d" % step), None, ALU.is_lt, None, ["pd" + s, "cthr%d" % step], ["ok" + s], W)
-        mms([(reg(u, 2), T.PAT[:], un("AT", u), True, False), (reg(u, 2), T["TRI%d" % t][:], un("ok", u), False, True)],
-            ["PAT", "AT" + s, "TRI%d" % t, "ok" + s], ["pc" + s], W)
+        ts(un("ok", u), T["pd" + s][:, 0:W], col("thr%d" % step) if step else 68.0, None, ALU.is_lt, None,
+           ["pd" + s] + (["cthr%d" % step] if step else []), ["ok" + s], W)
+        mms([(reg(u, 2), T.IDh[:], un("AT", u), True, False), (reg(u, 2), T["TRI%d" % t][:], un("ok", u), False, True)],
+            ["IDh", "AT" + s, "TRI%d" % t, "ok" + s], ["pc" + s], W)
         ts(un(k, u), reg(u, 2), -2.0 * LOW, -float(LOW), ALU.add, ALU.max, ["pc" + s], [k + s], W)
-        mms([(reg(u, 3), T.BOh[:], un(k, u), True, True)], ["BOh", k + s], ["pc" + s], W)
-        own("sc", u, 3)
-        ts(lst_(u, 0, 1), last16("sc", u), col("oNL"), None, ALU.add, None, ["sc" + s, "coNL"], ["NL" + s], WB)
+        if step < S - 1:
+            mms([(reg(u, 3), T.BOh[:], un(k, u), True, True)], ["BOh", k + s], ["pc" + s], W)
+            own("sc", u, 3)
+            ts(tab("NL", u), last16("sc", u), col("oNL"), None, ALU.add, None, ["sc" + s, "coNL"], ["NL" + s], WB)
+        else:
+            mms([(reg(u, 3), T.IDh[:], T.MKs[:], True, False), (reg(u, 3), T.BOh[:], un(k, u), False, True),
+                 (reg(u, 1), T.BOh[:], un(k, u), True, True)], ["IDh", "MKs", "BOh", k + s], ["pc" + s], W)
+            scan(un("sc", u), T.D1[:], reg(u, 3), BIG, ALU.min, ALU.max, ["D1", "pc" + s], ["sc" + s], W)
+            ts(tab("NL", u), last16("sc", u), float(CEN + B), None, ALU.add, None, ["sc" + s], ["NL" + s], WB)
 
     peers = [T.cores[q] for q in range(NR) if q != rank]
 
-    def finish(t, u, keys):
+    def finish(t, u, j, keys):
         s = str(u)
-        z, zk = zap(u, S - 1)
-        act(un("yg", u), xw(t).indirect(lst_(u, 0, 1)), ACT.Identity, 160.0, 1.0, keys + ["NL" + s], ["yg" + s], W, GAT)
-        ts(un("vb", u), reg(u, 3), 15.0 * LOW, None, ALU.add, None, ["pc" + s], ["vb" + s], W)
-        ts(tab("vT", u), last16("sc", u), col("ovT"), None, ALU.add, None, ["sc" + s, "covT"], ["vT" + s], WB)
-        tt(un("gt", u), un("yg", u), z, ALU.is_gt, ["yg" + s, zk], ["gt" + s], W)
-        mms([(reg(u, 4), T.BOb[:], un("gt", u), True, True)], ["BOb", "gt" + s], ["pc" + s], W)
-        own("sv", u, 4)
-        ts(tab("wt", u), last16("sv", u), col("ovo"), 2.0 ** -30, ALU.is_lt, ALU.add, ["sv" + s, "covo"], ["wt" + s], WB)
+        act(un("yg", u), xw(t).indirect(tab("NL", u)), ACT.Identity, 160.0, 1.0, keys + ["NL" + s], ["yg" + s], W, GAT)
+        if j >= GV:
+            tt(un("gt", u), xw(t).indirect(tab("NL", u)), un("zr", u), ALU.is_gt, keys + ["NL" + s, "zr" + s], ["gt" + s], W, 1, GAT)
+        else:
+            tt(un("gt", u), un("yg", u), un("z", u), ALU.is_gt, ["yg" + s, "z" + s], ["gt" + s], W)
+        ts(un("vb", u), reg(u, 1), 15.0 * LOW, None, ALU.add, None, ["pc" + s], ["vb" + s], W)
+        mms([(reg(u, 4), T.IDb[:], T.MKv[:], True, False), (reg(u, 4), T.BOn[:], un("gt", u), False, True)],
+            ["IDb", "MKv", "BOn", "gt" + s], ["pc" + s], W)
+        scan(un("sv", u), T.D2[:], reg(u, 4), BIG, ALU.min, ALU.max, ["D2", "pc" + s], ["sv" + s], W)
         d = (u - rank) % NR
-        halve(un("zt", u), u, d, un("yg", u), "yg" + s, z, zk, "zt" + s)
+        turn = T.PH[:, 128 - 16 * d:256 - 16 * d]
+        mms([(reg(u, 0), turn, un("z", u), True, False), (reg(u, 0), turn, un("yg", u), False, True)], ["PH", "yg" + s, "z" + s], ["pc" + s], W)
+        act(un("zt", u), reg(u, 0), ACT.Identity, 1.0, 1.0, ["pc" + s], ["zt" + s], W)
         if t == RO - 1:
-            act(un("vout", u), reg(u, 3), ACT.Identity, 15.0 * LOW + CEN, 1.0, ["pc" + s], ["vout" + s], W)
+            act(un("vout", u), reg(u, 1), ACT.Identity, 15.0 * LOW + CEN, 1.0, ["pc" + s], ["vout" + s], W)
         if d == 0:
             c0 = B + W0N + K * t + W * rank
             act(T.X[:, c0:c0 + W], un("zt", u), ACT.Identity, -160.0, 1.0, ["zt" + s], ["Xo%d" % t], W)
@@ -398,76 +389,94 @@ def rank_program(g, core, T, topo):
             act(T.snd[:, W * k:W * k + W], un("zt", u), ACT.Identity, -160.0, 1.0, ["zt" + s], ["snd%d" % k], W)
         act(un("VX", u), un("yg", u), ACT.Identity, col("fb"), col("fs"), ["yg" + s, "cfb", "cfs"], ["VX" + s], W)
 
-    def after(t, u):
+    def after(t, u, j):
         s = str(u)
-        prep(t, u)
+        if j < NLATE:
+            prep(t, u)
+        else:
+            ts(un("AT", u), aw(t).indirect(tab("NL", u)), -float(CEN), None, ALU.add, None, AK + ["NL" + s], ["AT" + s], W, 1, GAT)
         mms([(reg(u, 5), T.IDh[:], un("AT", u), True, False), (reg(u, 5), T.IDh[:], un("NW%d" % t, u), False, True)],
             ["IDh", "AT" + s, "NW%d" % t], ["pc" + s], W)
         act(un("VA", u), reg(u, 5), ACT.Identity, col("va%d" % t), 1.0, ["pc" + s, "cva%d" % t], ["VA" + s], W)
         c0 = B + W0N + K * t + W * u
         ts(T.A[:, c0:c0 + W], un("AT", u), col("m15"), col("nw15"), ALU.mult, ALU.add, ["AT" + s, "cm15", "cnw15"], ["An%d%s" % (t, s)], W)
 
-    def send(t):
+    def send(t, units, last):
         used = []
-        trs = [None] * len(peers)
+        trs = []
         c0 = B + W0N + K * t + W * rank
-        for k in sorted(range(len(peers)), key=lambda k: topo.chip(peers[k]) == topo.chip(core)):
+        ks = [u if u < rank else u - 1 for u in units]
+        for k in sorted(ks, key=lambda k: len(topo.engines(core, peers[k]))):
             en = [e for e in topo.engines(core, peers[k]) if e not in used][:ENG]
             used += en
             rid, pid = topo.addr(peers[k])[:2]
-            trs[k] = RemoteDMATransfer(dst_ids=[DstId(rid=rid, pnc=pid)], dma_engine_mask=sum(1 << e for e in en),
-                                       remote_sem=T.sem["arr%d" % t], src=T.snd[:, W * k:W * k + W], dst=T.X[:, c0:c0 + W])
-        rec("G", "send", lambda: g.remote_dma_fused(trs, local_sem=T.sem.snt), ["snd%d" % k for k in range(len(peers))],
-            ["Xa%d" % t], 1.5, 4.0, "arr%d" % t)
+            trs.append(RemoteDMATransfer(dst_ids=[DstId(rid=rid, pnc=pid)], dma_engine_mask=sum(1 << e for e in en),
+                                         remote_sem=T.sem["arr%d" % t], src=T.snd[:, W * k:W * k + W], dst=T.X[:, c0:c0 + W]))
+        rec("G", "send", lambda: g.remote_dma_fused(trs, local_sem=T.sem["snt%d" % last]), ["snd%d" % k for k in ks],
+            ["Xa%d" % t if last else "Xb%d" % t], 1.2, 4.0, ("arr%d" % t, "snt%d" % last, ENG * len(ks)))
 
-    half = NU // 2
-    mine = [u for u in range(NU) if u // half == rank // half]
-    ORD = [u for u in range(NU) if u not in mine] + [u for u in mine if u != rank] + [rank]
-    PX = "pd%d" % ORD[0]
+    ORD = sorted(range(NU), key=lambda u: (u == rank, topo.chip(T.cores[u]) == topo.chip(core), u))
+    LAST = NU - 1
+    CUT = W * LAST
+    PX, PA, PY = ("pd%d" % u for u in ORD[:3])
 
-    def pairs(t, u, c0, c1, last):
-        mats = ("FB", "MT", "NB") if t == RO - 1 else ("FS", "MS", "NB")
-        for k in range(WB * u, WB * u + WB):
-            e = "EQ%d_%d" % (k, c0)
-            ts(T.EQ[:, 256 * k + c0:256 * k + c1], T.vb[:, c0:c1], T.vT[:, k:k + 1], T.wt[:, k:k + 1], ALU.is_equal, ALU.mult,
-               ["vb%d" % v for v in range(c0 // W, c1 // W)] + ["vT%d" % u, "wt%d" % u], [e], c1 - c0, 0.5)
-            a, b = 16 * k, 16 * k + 16
-            lst = [(lo, hi, m) for (lo, hi), m in zip(((c0, min(a, c1)), (a, b), (max(b, c0), c1)), mats) if c0 <= lo < hi <= c1]
-            mms([(T[PX][:, lo:hi], T[m][:], T.EQ[:, 256 * k + lo:256 * k + hi], False, last and k == WB * u + WB - 1 and i == len(lst) - 1)
-                 for i, (lo, hi, m) in enumerate(lst)], [m for _, _, m in lst] + [e], [PX],
-                sum(max(64, hi - lo) for lo, hi, _ in lst) / len(lst))
-
-    def opened(c0, c1, start):
-        lst = [(T[PX][:, 0:K], T.IDh[:], T.MK0[:], True, False)] if start else []
-        mms(lst + [(T[PX][:, c0:c1], T.IDh[:], T.vb[:, c0:c1], False, False)],
-            ["IDh", "MK0"] + ["vb%d" % v for v in range(c0 // W, c1 // W)], [PX], 192 if start else c1 - c0)
+    def ranges(ps, k, a, b):
+        p, out = k // WB, []
+        for q in range(a, b):
+            lo, hi = W * q, W * q + W
+            if ps == PA:
+                new = [(16 * k, 16 * k + 16, "MA"), (16 * k + 16, hi, "NB")] if q == p else [(lo, hi, "NB")] if ORD[p] < ORD[q] else []
+            elif (q == LAST) != (ps == PY):
+                new = []
+            elif q != p and LAST in (p, q):
+                new = [(lo, hi, "NB" if p == LAST else "FB")]
+            else:
+                new = [(lo, min(hi, 16 * k + 16), "MT"), (max(lo, 16 * k + 16), hi, "MU")]
+            for lo, hi, m in new:
+                if lo < hi:
+                    if out and out[-1][1:] == (lo, m):
+                        lo = out.pop()[0]
+                    out.append((lo, hi, m))
+        return out
 
     def joint(t, j):
-        def hf(u):
-            return (K // 2 * (u // half), K // 2 * (u // half) + K // 2)
+        jobs = [(k, a, b) for p, a, b in PAIRS.get(j, []) for k in range(WB * p, WB * p + WB)]
+        for k, a, b in jobs:
+            u = ORD[k // WB]
+            plain = (k // WB, a) == (LAST, 0)
+            ts(T.EQ[:, K * k + W * a:K * k + W * b], T.vb[:, W * a:W * b], T.sc[:, 16 * k + 15:16 * k + 16],
+               1.0 if plain else T.sv[:, 16 * k + 15:16 * k + 16], ALU.is_equal, ALU.min,
+               ["vb%d" % v for v in ORD[a:b]] + ["sc%d" % u] + ([] if plain else ["sv%d" % u]), ["EQ%d_%d" % (k, a)], W * (b - a), 0.5)
+        if j:
+            sums(PX, jobs, {1: (0, 2), 2: (2, 3)}.get(j), j == 1, j == LAST)
+        if j == LAST:
+            sums(PY, jobs, (LAST, NU), True, True)
+            if t < RO - 1:
+                sums(PA, [(k, a, b) for i in PAIRS for p, a, b in PAIRS[i] for k in range(WB * p, WB * p + WB)], (0, NU), True, True)
 
-        def one(u):
-            return (W * u, W * u + W)
-        h0, h1 = hf(ORD[0]), hf(ORD[-1])
-        if j == 0:
-            return
-        if j == 1:
-            opened(h0[0], h0[1], True)
-            todo = [(ORD[0], h0), (ORD[1], h0)]
-        elif not FINE:
-            if j == 3:
-                opened(h1[0], h1[1], False)
-            todo = [(ORD[2], h0)] if j == 2 else [(ORD[0], h1), (ORD[1], h1), (ORD[2], h1), (ORD[3], (0, K))]
-        else:
-            opened(W * ORD[j], W * ORD[j] + W, False)
-            todo = [(u, one(ORD[j])) for u in ORD[:j]]
-            todo += [(ORD[2], h0), (ORD[2], one(ORD[2]))] if j == 2 else [(ORD[3], (0, K))]
-        for i, (u, c) in enumerate(todo):
-            pairs(t, u, c[0], c[1], j == 3 and i == len(todo) - 1)
+    def span(ps):
+        return {PX: (0, CUT), PY: (CUT, K), PA: (0, K)}[ps]
 
-    def places(off):
-        op("V", lambda: g.vector.tensor_tensor_scan(T.scX[:], T.D0[:], T[PX][:, 0:K], 1e9, ALU.min, ALU.max), ["D0", PX], ["scX"], vd(K))
-        ts(T[off][:], T.scX[:, 15:K:16], CEN + B - LIFT + 0.3, None, ALU.add, None, ["scX"], [off], 16)
+    def sums(ps, jobs, base, first, last):
+        c0, c1 = span(ps)
+        if first:
+            mms([(T[ps][:, c0:c1], T.IDh[:], T.MK0[:, c0:c1], True, False)], ["IDh", "MK0"], [ps, "~" + ps], c1 - c0)
+        if base:
+            mms([(T[ps][:, W * base[0]:W * base[1]], T.IDh[:], T.vb[:, W * base[0]:W * base[1]], False, False)],
+                ["IDh", "~" + ps] + ["vb%d" % v for v in ORD[base[0]:base[1]]], [], W * (base[1] - base[0]))
+        jobs = [(k, a, ranges(ps, k, a, b)) for k, a, b in jobs if ranges(ps, k, a, b)]
+        for i, (k, a, lst) in enumerate(jobs):
+            end = last and i == len(jobs) - 1
+            mms([(T[ps][:, lo:hi], T[m][:], T.EQ[:, K * k + lo:K * k + hi], False, end and lo == lst[-1][0]) for lo, hi, m in lst],
+                [m for _, _, m in lst] + ["EQ%d_%d" % (k, a), "~" + ps] + (["~X"] if ps == PA and AFTER else []),
+                [ps, "~" + ps, "~X"] if end else [], sum(max(64, hi - lo) for lo, hi, _ in lst) / len(lst))
+
+    def places(ps, sc, off):
+        c0, c1 = span(ps)
+        scan(T[sc][:, c0:c1], T.D0[:, c0:c1], T[ps][:, c0:c1], BIG, ALU.min, ALU.max, ["D0", ps] + (["~S"] if ps == PA else []),
+             [sc + ps], c1 - c0)
+        ts(T[off][:, c0 // 16:c1 // 16], T[sc][:, c0 + 15:c1:16], CEN + B + 0.25, None, ALU.add, None, [sc + ps], [off + ps], 16)
+        return T[off][:, c0 // 16:c1 // 16]
 
     old = XK
     for t in range(RO):
@@ -476,46 +485,42 @@ def rank_program(g, core, T, topo):
                 stage[0] = 1 + j
                 prep(t, u)
         else:
-            old, XK = XK, XK + ["Xa%d" % (t - 1), "Xo%d" % (t - 1)]
+            old, XK = XK, XK + ["Xa%d" % (t - 1), "Xb%d" % (t - 1), "Xo%d" % (t - 1)]
         for st in range(S):
             for j, u in enumerate(ORD):
                 stage[0] = 20 * t + 1 + NU * st + j
-                bulk(t, u, st, old, XK)
+                bulk(t, u, st, j, old, XK)
                 choose(t, u, st)
                 if st < S - 1:
                     prep(t, u)
+                    advance(t, u, st + 1, XK, j)
                 else:
-                    finish(t, u, XK)
+                    finish(t, u, j, XK)
+                    if j == NU - 3 and SPLIT:
+                        send(t, ORD[:j + 1], 0)
                     if j == NU - 2:
-                        send(t)
+                        send(t, ORD[j:j + 1] if SPLIT else ORD[:j + 1], 1)
                     stage[0] = 20 * t + 16.5
                     joint(t, j)
                     if t < RO - 1:
                         stage[0] = 20 * t + 16.7
-                        after(t, u)
+                        after(t, u, j)
             if t == RO - 1 and st == 0:
                 dma("Y", T.yx[1:128:2, 0:AC - B], T.X[1:128:2, B:AC], "dE", XK, [], 5.0)
         stage[0] = 20 * t + 16.6
-        if t == RO - 1:
-            places("OFX")
-        else:
-            ts(T.vX[:], T.vT[:], float(LIFT), None, ALU.add, None, ["vT%d" % u for u in range(NU)], ["vX"], 16)
-            places("OFA")
-            tt(T.fe[:], T.scX[:, 15:K:16], T.vX[:], ALU.is_equal, ["scX", "vX"], ["fe"], 16)
-            tt(T.fm[:], T.fe[:], T.vX[:], ALU.mult, ["fe", "vX"], ["fm"], 16)
-            tt(T.fo[:], T.fm[:], T.D0[:, 0:K:16], ALU.max, ["fm", "D0"], ["fo"], 16)
-            ts(T.OFX[:], T.fo[:], float(CEN + B - LIFT), None, ALU.add, None, ["fo"], ["OFX"], 16)
-        cp(xw(t).indirect(T.OFX[:]), T.VX[:], ["VX%d" % u for u in range(NU)] + ["OFX"], XK, K, SCA)
+        for ps, us in ((PX, ORD[:LAST]), (PY, ORD[LAST:])):
+            c0, c1 = span(ps)
+            cp(xw(t).indirect(places(ps, "scX", "OFX")), T.VX[:, c0:c1], ["VX%d" % u for u in us] + ["OFX" + ps], XK + ["~S"], c1 - c0, SCA)
         if t < RO - 1:
             stage[0] = 20 * t + 17
-            cp(aw(t).indirect(T.OFA[:]), T.VA[:], ["VA%d" % u for u in range(NU)] + ["OFA"], AK, K, SCA)
+            cp(aw(t).indirect(places(PA, "scA", "OFA")), T.VA[:], ["VA%d" % u for u in range(NU)] + ["OFA" + PA], AK, K, SCA)
             AK = AK + ["An%d%d" % (t, u) for u in range(NU)]
     dma("Y", T.yx[0:128:2, 0:AC - B], T.X[0:128:2, B:AC], "dO", XK, [], 4.0)
-    dma("Y", T.yx[:, AC - B:XC - B], T.X[:, AC:XC], "dO", ["Xa%d" % (RO - 1), "Xo%d" % (RO - 1)], [], 2.0)
+    dma("Y", T.yx[:, AC - B:XC - B], T.X[:, AC:XC], "dO", ["Xa%d" % (RO - 1), "Xb%d" % (RO - 1), "Xo%d" % (RO - 1)], [], 2.5)
     dma("Y", T.yv[:], T.vout[0:128:16, :], "dO", ["vout%d" % u for u in range(NU)], [], 2.0)
 
     n = len(recs)
-    preds = [set() for _ in range(n)]
+    preds = [{} for _ in range(n)]
     lw, lr = {}, {}
 
     def bank(k):
@@ -523,54 +528,58 @@ def rank_program(g, core, T, topo):
 
     for i, r in enumerate(recs):
         reads, writes = r[3], r[4]
+        for k in reads + writes:
+            for j in ([lw[k]] if k in lw else []) + (lr.get(k, []) if k in writes else []):
+                preds[i][j] = preds[i].get(j, False) or not (k[0] in "p~" and recs[j][0] == r[0])
         for k in reads:
-            if k in lw:
-                preds[i].add(lw[k])
             lr.setdefault(k, []).append(i)
-        for k in writes:
-            if k in lw:
-                preds[i].add(lw[k])
-            preds[i].update(lr.get(k, []))
         for k in reads + writes:
             if bank(k) or k in writes:
                 lw[k] = i
                 lr[k] = []
-        preds[i].discard(i)
+        preds[i].pop(i, None)
     succ = [[] for _ in range(n)]
     for i in range(n):
         for j in preds[i]:
             succ[j].append(i)
     prio = [0.0] * n
     for i in range(n - 1, -1, -1):
-        prio[i] = recs[i][5] + recs[i][6] + max([prio[j] + WK for j in succ[i]], default=0.0)
-    left = [len(p) for p in preds]
-    ready = [0.0] * n
-    avail = {q: [] for q in QUE}
-    for i in range(n):
-        if left[i] == 0:
-            avail[recs[i][0]].append(i)
-    tq = {q: 0.0 for q in QUE}
-    order = []
-    while len(order) < n:
-        best = None
-        for q in QUE:
-            if avail[q]:
-                e = min(max(tq[q], ready[i]) for i in avail[q])
-                if best is None or e < best[0]:
-                    best = (e, q)
-        e, q = best
-        c = [i for i in avail[q] if max(tq[q], ready[i]) <= e + LOOK]
-        i = max(c, key=lambda j: (-recs[j][8], prio[j], -j))
-        avail[q].remove(i)
-        tq[q] = max(tq[q], ready[i]) + recs[i][5]
-        end = tq[q] + recs[i][6]
-        order.append(i)
-        for j in succ[i]:
-            same = recs[j][0] == q == "P"
-            ready[j] = max(ready[j], tq[q] if same else end + WK)
-            left[j] -= 1
-            if left[j] == 0:
-                avail[recs[j][0]].append(j)
+        prio[i] = recs[i][5] + recs[i][6] + max([prio[j] + WK * preds[j][i] for j in succ[i]], default=0.0)
+
+    def schedule(before, behind, key, back):
+        left = [len(p) for p in before]
+        ready = [0.0] * n
+        start = [0.0] * n
+        avail = {q: [] for q in QUE}
+        for i in range(n):
+            if left[i] == 0:
+                avail[recs[i][0]].append(i)
+                ready[i] = recs[i][6] if back else 0.0
+        tq = {q: 0.0 for q in QUE}
+        order = []
+        while len(order) < n:
+            e, q = min((min(max(tq[q], ready[i]) for i in avail[q]), q) for q in QUE if avail[q])
+            i = max((i for i in avail[q] if max(tq[q], ready[i]) <= e + LOOK[q]), key=key)
+            avail[q].remove(i)
+            start[i] = max(tq[q], ready[i])
+            tq[q] = start[i] + recs[i][5]
+            order.append(i)
+            for j in behind[i]:
+                hard = preds[i][j] if back else preds[j][i]
+                ready[j] = max(ready[j], tq[q] + (recs[j if back else i][6] + WK if hard else 0.0))
+                left[j] -= 1
+                if left[j] == 0:
+                    avail[recs[j][0]].append(j)
+        return max(start[i] + recs[i][5] + (0 if back else recs[i][6]) for i in range(n)), order, start
+
+    best = cur = schedule(preds, succ, lambda j: (-recs[j][8], prio[j], -j), False)
+    for _ in range(TURNS):
+        fw = cur[2]
+        bw = schedule(succ, preds, lambda j: fw[j] + recs[j][5], True)[2]
+        cur = schedule(preds, succ, lambda j: (-min(recs[j][8], 1), -j if recs[j][1] == "dma" else bw[j] + recs[j][5]), False)
+        if cur[0] < best[0]:
+            best = cur
+    order = best[1]
 
     cnt = {}
     known = {q: {} for q in QUE}
@@ -593,6 +602,7 @@ def rank_program(g, core, T, topo):
             total[r[7]] = total.get(r[7], 0) + 16
     for i in order:
         q, kind, fn, reads, writes, dur, lat, sem, stg = recs[i]
+        reads, writes = [k for k in reads if k[0] != "~"], [k for k in writes if k[0] != "~"]
         toks = []
         for k in reads:
             if bank(k):
@@ -618,11 +628,11 @@ def rank_program(g, core, T, topo):
             who = q + sem
         else:
             fn()
-            cnt["snt"] = cnt.get("snt", 0) + ENG * len(peers)
-            rtok = ("snt", cnt["snt"], dict(known[q]))
+            sem, who, m = sem
+            cnt[who] = cnt.get(who, 0) + m
+            rtok = (who, cnt[who], dict(known[q]))
             cnt[sem] = ENG * len(peers)
             tok = (sem, cnt[sem], {})
-            who = "rem"
         for k in writes:
             if bank(k):
                 lastr.setdefault(k, {})[q] = tok

import numpy as np
from concourse.bass import DstId, RemoteDMATransfer
from concourse.mybir import AluOpType, ActivationFunctionType

ALU = AluOpType
ACT = ActivationFunctionType

W0N, K, RO, S = 3072, 256, 3, 4
NU = 4
W = K // NU
WB = W // 16
B = 384
CEN = 1919
LOW = 2048
HOLD = 8192
BIG = 2.0 ** 23
PG = 2
XG = 2
ZQ = "V"
ZP = True
HELP = 32
PAIRS = {1: [(0, 0, 2), (1, 0, 2)], 2: [(2, 0, 3)], 3: [(0, 2, 4), (1, 2, 4), (2, 3, 4), (3, 0, 3), (3, 3, 4)]}
XC = B + W0N + RO * K
AC = B + W0N + (RO - 1) * K
CYC = 0.00083
PEC = 0.00042
GAT = 1.56
NLATE = 2
GV = 3
SCA = 3.8
WK = 0.26
TURNS = 3
SOFT = 1
AFTER = True
SPLIT = False
LOOK = {"V": 0.02, "S": 0.02, "P": 0.02, "G": 0.02, "Y": 0.02}
LATE = 0.5
ENG = 4

SCRATCH = {}


def _b(name, cols, dtype, where="sbuf"):
    SCRATCH[name] = (where, [128, cols], dtype)


_b("X", XC, "bfloat16")
_b("A", AC, "int32")
_b("WL", 16, "int32")
for _n in ("NL", "LL", "OFA", "OFX"):
    _b(_n, 16, "uint16")
for _n in ("z", "zr", "zt", "s", "xl", "ok", "gt", "yg", "VX", "J", "J2", "JM", "PH", "ta", "tb", "tc", "te", "tf"):
    _b(_n, 256, "bfloat16")
for _n in ("AT", "sA0", "sA1", "sA2", "sA3", "vb", "MK0", "NW0", "NW1"):
    _b(_n, 256, "float16")
_b("LT", 256, "uint16")
_b("xg", 16 * 256, "bfloat16")
_b("mn", 15 * 256, "bfloat16")
for _u in range(NU):
    _b("pd%d" % _u, 512, "float32", "psum")
    _b("pc%d" % _u, 512, "float32", "psum")
_b("EQ", 16 * 256, "bfloat16")
for _n in ("sc", "sv", "scX", "scA", "VA", "vout", "JC", "D0"):
    _b(_n, 256, "float32")
for _n in ("M", "D1", "D2", "JB"):
    _b(_n, W, "float32")
_b("MKs", W, "float16")
_b("MKv", W, "bfloat16")
_b("snd", 192, "bfloat16")
_b("PI", 8, "int32")
_b("PJ", 16, "float32")
_b("col", 64, "float32")
_b("W1", 144, "bfloat16")
_b("W2", 144, "bfloat16")
for _n in ("JG", "JP", "BOb", "BOn", "NB", "FB", "MT", "MU", "MA", "ZS", "IDb", "TRI0", "TRI1", "TRI2"):
    _b(_n, 128, "bfloat16")
for _n in ("BOh", "IDh", "DEAD", "RW0", "RW1"):
    _b(_n, 128, "float16")

SEMAPHORES = ["qV", "qS", "qP", "qG", "dX", "dW", "dA", "dO", "dE", "arr0", "arr1", "arr2", "snt0", "snt1"]


def rank_program(g, core, T, topo):
    rank = T.rank_of(core)
    if rank is None:
        return
    NR = len(T.cores)
    QUE = {"V": g.vector, "S": g.scalar, "P": g.tensor, "G": g, "Y": g.sync}
    recs = []
    stage = [0]

    def rec(q, kind, fn, reads, writes, dur, lat=0.0, sem=None):
        recs.append((q, kind, fn, tuple(reads), tuple(writes), dur, lat, sem, stage[0]))

    def op(q, fn, reads, writes, dur):
        rec(q, "op", fn, reads, writes, dur)

    def dma(q, out, in_, sem, reads, writes, lat):
        rec(q, "dma", lambda: QUE[q].dma_start(out, in_), reads, writes, 0.06, lat, sem)

    def vd(n, f=1.0, ind=None):
        return max(64, n * f) * CYC if ind is None else 0.05 + n * CYC * ind

    def ts(out, in0, s1, s2, op0, op1, reads, writes, n=128, f=1.0, ind=None):
        if op1 is None:
            op("V", lambda: g.vector.tensor_scalar(out, in0, s1, s2, op0), reads, writes, vd(n, f, ind))
        else:
            op("V", lambda: g.vector.tensor_scalar(out, in0, s1, s2, op0, op1), reads, writes, vd(n, f, ind))

    def tt(out, in0, in1, o, reads, writes, n=128, f=1.0, ind=None):
        op("V", lambda: g.vector.tensor_tensor(out, in0, in1, o), reads, writes, vd(n, f, ind))

    def cp(out, in_, reads, writes, n, ind=None):
        op("V", lambda: g.vector.tensor_copy(out, in_), reads, writes, vd(n, 1.0, ind))

    def scan(out, d0, d1, init, op0, op1, reads, writes, n):
        op("V", lambda: g.vector.tensor_tensor_scan(out, d0, d1, init, op0, op1), reads, writes, vd(n))

    def act(out, in_, f, bias, scale, reads, writes, n=128, ind=1.0):
        op("S", lambda: g.scalar.activation(out, in_, f, bias=bias, scale=scale), reads, writes, 0.065 + n * CYC * ind)

    def mms(lst, reads, writes, n=128):
        def go():
            r = None
            for (o, l, r_, st, sp) in lst:
                r = g.tensor.matmul(o, l, r_, st, sp)
            return r
        op("P", go, reads, writes, len(lst) * max(n, 64) * PEC)

    stage[0] = -1
    dma("Y", T.WL[:], T.w0[:], "dW", [], ["WL"], 3.0)
    stage[0] = 0
    dma("S", T.A[15:128:16, B:B + W0N], T.nx[:], "dA", [], ["A8"], 6.0)
    for gr in range(8):
        dma("S" if gr % 2 else "Y", T.A[16 * gr:16 * gr + 15, B:B + W0N], T.lk[16 * gr:16 * gr + 15, :], "dA", [], ["A%d" % gr], 6.0)
    stage[0] = 0.1
    dma("Y", T.X[:, B:B + W0N], T.x0[:], "dX", [], ["X"], 7.5)
    stage[0] = 0
    AK = ["A%d" % i for i in range(9)] + ["Am"]
    XK = ["X", "Xm"]

    CI = {}

    def newcol(name):
        CI[name] = len(CI)
        return col(name)

    def col(name):
        if name[0] == "P":
            i = int(name[1:]) // 16 + 7
            return T.PJ[:, i:i + 1]
        i = CI[name]
        return T.col[:, i:i + 1]

    def iota(ap, key, pattern, base, cm, n, whole=False):
        if whole:
            op("G", lambda: g.iota(ap, pattern, base, cm), [], [key], 0.13 + 2 * CYC * n)
        else:
            op("G", lambda: g.iota(ap, pattern, base, cm, allow_small_or_imprecise_dtypes=True), [], [key], 0.13 + 2 * CYC * n)

    def ck(name):
        return "PJ" if name[0] == "P" else "c" + name

    def sc_(s):
        return col(s) if isinstance(s, str) else s

    def mkcol(name, src, s1, s2, op0, op1):
        in0, key = (T.PI[:, src:src + 1], "PI%d" % src) if isinstance(src, int) else (col(src), ck(src))
        ts(newcol(name), in0, sc_(s1), sc_(s2), op0, op1, [key] + [ck(s) for s in (s1, s2) if isinstance(s, str)], ["c" + name], 1)

    def mat(out, src, s1, s2, op0, op1, n=128, f=0.5):
        ts(T[out][:, 0:n], T[src][:, 0:n], sc_(s1), sc_(s2), op0, op1, [src] + [ck(s) for s in (s1, s2) if isinstance(s, str)], [out], n, f)

    def mat2(out, a, b, o, n=128, f=1.0):
        tt(T[out][:, 0:n], T[a][:, 0:n], T[b][:, 0:n], o, [a, b], [out], n, f)

    iota(T.PI[:, 0:1], "PI0", [[0, 1]], 0, 1, 1, True)
    iota(T.PJ[:], "PJ", [[16, 16]], -112, 1, 16)
    iota(T.JG[:], "JG", [[16, 8], [0, 16]], 0, 0, 128)
    iota(T.JM[:], "JM", [[0, 16], [1, 16]], 0, 0, 256)
    iota(T.J[:], "J", [[1, 256]], 0, 0, 256)
    op("V", lambda: g.vector.memset(T.A[:, 0:B], -1), [], ["Am"], vd(B))
    op("V", lambda: g.vector.memset(T.X[:, 0:B], 95.0), [], ["Xm"], vd(B, 0.5))
    for i, m in ((1, 15), (3, 1)):
        ts(T.PI[:, i:i + 1], T.PI[:, 0:1], m, None, ALU.bitwise_and, None, ["PI0"], ["PI%d" % i], 1)
    mkcol("R", 1, 0.0, None, ALU.add, None)
    mkcol("G", "R", -1.0, "P0", ALU.mult, ALU.add)
    mkcol("G15", "G", 15.0, None, ALU.add, None)
    mkcol("m15", "R", 15.0, None, ALU.is_equal, None)
    mkcol("RP", "m15", -16.0, "R", ALU.mult, ALU.add)
    for k in range(1, S):
        mkcol("thr%d" % k, "RP", -float(LOW * k), 68.0 - LOW * k, ALU.mult, ALU.add)
    mkcol("r0", "R", 0.0, 2.0 * HOLD, ALU.is_equal, ALU.mult)
    mkcol("oNL", "r0", float(CEN + B + 15 * LOW - HOLD), None, ALU.add, None)
    mkcol("Rb", "r0", 8.0 / HOLD, -1.0, ALU.mult, ALU.add)
    mkcol("Rm", "Rb", "R", None, ALU.add, None)
    ts(T.NL[:], T.WL[:], float(B), None, ALU.add, None, ["WL"], ["NL%d" % u for u in range(NU)], 16)
    mat("BOb", "JG", "G", None, ALU.is_equal, None)
    mat("ta", "JM", 15.0, None, ALU.is_lt, None)
    mat2("ZS", "ta", "BOb", ALU.mult)
    mat("W1", "J", "G15", None, ALU.is_equal, None, 144)
    mat("W2", "J", "G15", -2.0, ALU.is_equal, ALU.mult, 144)
    mat("IDb", "J", "P0", None, ALU.is_equal, None)
    mat("IDh", "J", "P0", None, ALU.is_equal, None)
    mat("tb", "JM", 15.0, -16.0, ALU.is_equal, ALU.mult)
    mat2("JP", "tb", "JM", ALU.add)
    mat("ta", "JP", "RP", -2.0 * LOW, ALU.is_lt, ALU.mult)
    mat("tb", "JP", "RP", 2.0 * LOW, ALU.is_equal, ALU.mult)
    mat2("tc", "ta", "tb", ALU.add)
    mat2("te", "tc", "BOb", ALU.mult)
    for t in range(RO):
        stage[0] = LATE if t else 0
        mkcol("rv%d" % t, "RP", float(13 + t), None, ALU.is_lt, None)
        mat("tf", "JP", float(13 + t), "rv%d" % t, ALU.is_lt, ALU.mult)
        mat2("TRI%d" % t, "tf", "te", ALU.mult)
    stage[0] = 0
    mat("BOh", "JG", "G", None, ALU.is_equal, None)
    mat("ta", "JM", "R", float(HOLD), ALU.is_equal, ALU.mult, W)
    mat("tb", "JM", "Rm", -2.0 * HOLD, ALU.is_equal, ALU.mult, W)
    mat2("M", "ta", "tb", ALU.add, W, 2)
    mat("tc", "JM", "R", None, ALU.is_ge, None)
    mat2("DEAD", "tc", "ZS", ALU.mult)
    stage[0] = LATE
    HALF = 127.0 / 256
    iota(T.J2[:], "J2", [[0, 2], [1, 128]], 0, 0, 256)
    iota(T.JC[:], "JC", [[-16, 16], [0, 16]], 240 - CEN - B, 1, 256)
    iota(T.JB[:], "JB", [[0, W]], int(BIG), 0, W)

    def starts(out, src, n, keep, fill):
        op("G", lambda: g.affine_select(T[out][:], T[src][:], [[0, n // 16], [1, 16]], keep, fill, 0, 0), [src], [out], 0.17 + 2 * CYC * n)
    starts("D0", "JC", K, ALU.is_equal, BIG)
    starts("D1", "JB", W, ALU.not_equal, -2.0 * LOW)
    starts("D2", "JB", W, ALU.not_equal, 2.0 ** -30)
    mkcol("fs", 3, 2.0, -1.0, ALU.mult, ALU.add)
    mkcol("fb", 3, -335.0, 175.0, ALU.mult, ALU.add)
    mkcol("nw15", "m15", CEN + 1.0, -1.0, ALU.mult, ALU.add)
    mkcol("oLL", "r0", float(CEN + B - HOLD), None, ALU.add, None)
    mat("PH", "J2", "P0", HALF, ALU.is_equal, ALU.mult, 256)
    mat("MK0", "JM", "R", -float(HOLD), ALU.not_equal, ALU.mult, 256)
    mat("MKs", "MK0", 15.0 * LOW, None, ALU.add, None, W)
    mat("MKv", "MK0", 8.5, None, ALU.add, None, W)
    mat("BOn", "JG", "G", -1.0, ALU.is_equal, ALU.mult)
    mat("NB", "JG", "G", -2.0 ** 43, ALU.is_equal, ALU.mult)
    mat("FB", "JG", "G", -2.0 ** 14, ALU.is_equal, ALU.mult)
    mat("ta", "JM", "R", None, ALU.is_gt, None)
    mat2("MA", "ta", "NB", ALU.mult)
    mat2("MT", "MA", "FB", ALU.min)
    mat("tb", "JM", "R", None, ALU.is_ge, None)
    mat2("tc", "tb", "NB", ALU.mult)
    mat2("MU", "tc", "FB", ALU.min)
    for t in range(RO - 1):
        mkcol("rt%d" % t, "R", float(13 + t), None, ALU.is_equal, None)
        mkcol("va%d" % t, "rt%d" % t, 2048.0, float(CEN), ALU.mult, ALU.add)
        mat("NW%d" % t, "J", float(W0N + K * t + 1 - 2048), "rt%d" % t, ALU.add, ALU.mult, 256)
        mat("RW%d" % t, "JG", "G", "rt%d" % t, ALU.is_equal, ALU.mult)

    def un(name, u):
        if name in ("vb", "sc", "sv", "VX", "VA"):
            u = ORD.index(u)
        return T[name][:, W * u:W * u + W]

    def tab(name, u):
        return T[name][:, WB * u:WB * u + WB]

    def last16(name, u):
        u = ORD.index(u)
        return T[name][:, W * u + 15:W * u + W:16]

    def reg(u, k):
        return T["pc%d" % u][:, W * k:W * k + W]

    def xw(t):
        return T.X[:, 0:B + W0N + K * t]

    def aw(t):
        return T.A[:, 0:B + W0N + K * t]

    def own(out, u, k):
        scan(un(out, u), reg(u, k), T.M[:], -1e6, ALU.max, ALU.add, ["M", "pc%d" % u], [out + str(u)], W)

    def prep(t, u):
        s = str(u)
        ts(un("LT", u), aw(t).indirect(tab("NL", u)), float(B), None, ALU.add, None, AK + ["NL" + s], ["LT" + s], W, 1, GAT)
        ts(un("AT", u), un("LT", u), -float(B + CEN), None, ALU.add, None, ["LT" + s], ["AT" + s], W, 0.5)

    def newlist(t, u):
        s = str(u)
        ts(un("AT", u), aw(t).indirect(tab("NL", u)), -float(CEN), None, ALU.add, None, AK + ["NL" + s], ["AT" + s], W, 1, GAT)
        ps = "pd%d" % ORD[-1]
        mms([(T[ps][:, 0:W], T["RW%d" % t][:], un("AT", u), True, True)], ["RW%d" % t, "AT" + s], [ps], W)
        scan(un("sv", u), T[ps][:, 0:W], T.M[:], -1e6, ALU.max, ALU.add, ["M", ps], ["sv" + s], W)
        ts(tab("LL", u), last16("sv", u), col("oLL"), None, ALU.add, None, ["sv" + s, "coLL"], ["LL" + s], WB)

    def advance(t, u, step, keys, j):
        s = str(u)
        if step == 0:
            ts(un("z", u), xw(max(t - 1, 0)).indirect(tab("NL", u)), 160.0, None, ALU.add, None, keys + ["NL" + s], ["z" + s], W, 1, GAT)
        else:
            tt(un("s", u), xw(t).indirect(tab("NL", u)), un("z", u), ALU.add, keys + ["NL" + s, "z" + s], ["s" + s], W, 1, GAT)
            if ZQ == "V":
                ts(un("z", u), un("s", u), 0.5, 79.75, ALU.mult, ALU.add, ["s" + s], ["z" + s], W, 0.5)
            else:
                act(un("z", u), un("s", u), ACT.Identity, 79.75, 0.5, ["s" + s], ["z" + s], W)
        if ZP:
            mms([(reg(u, 7), T.IDb[:], un("z", u), True, True)], ["IDb", "z" + s], ["pc" + s], W)
        if step == S - 1 and j >= GV:
            act(un("zr", u), un("z", u), ACT.Identity, -160.0, 1.0, ["z" + s], ["zr" + s], W)

    def bulk(t, u, step, j, old, new):
        s = str(u)
        nl = 13 + t
        late = step == 0 and t > 0 and j < NLATE
        pd = T["pd" + s][:, 0:W]
        o = 16 * W * u
        win, keys = (xw(t - 1), old) if late else (xw(t), new)
        if step == 0:
            if t and not late:
                prep(t - 1, u)
            advance(t, u, step, old, j)
        n = HELP if step == 0 and j == 0 and t == 0 else 0
        if n:
            ts(T.xg[:, o:o + 16 * n], win.indirect(T.LT[:, W * u:W * u + n]), 160.0, None, ALU.add, None, keys + ["LT" + s], ["xh" + s],
               16 * n, 1, GAT)
        act(T.xg[:, o + 16 * n:o + 16 * W], win.indirect(T.LT[:, W * u + n:W * u + W]), ACT.Identity, 160.0, 1.0,
            keys + ["LT" + s] + (["~L"] if j > 1 else []),
            ["xg" + s] + ([] if n else ["xh" + s]), 16 * (W - n), GAT)
        mms([(pd, T.DEAD[:], un("sA%d" % k, u), k == 0, False) for k in range(step)] + [(pd, T.ZS[:], un("z", u), step == 0, False)],
            ["ZS", "z" + s, "DEAD"] + ["sA%d%s" % (k, s) for k in range(step)], ["pd" + s], W)
        if late:
            newlist(t - 1, u)
        z, zk = (reg(u, 7), "pc" + s) if ZP else (un("z", u), "z" + s)

        def part(a, b, x, xk):
            for c in range(a, b, XG):
                mms([(pd, T.W1[:, 15 - i:143 - i], x(i), False, False) for i in range(c, min(b, c + XG))], ["W1"] + xk, ["pd" + s], W)
            for c in range(a, b, PG):
                d = min(b, c + PG)
                for i in range(c, d):
                    tt(T.mn[:, W * (15 * u + i):W * (15 * u + i + 1)], x(i), z, ALU.min, [zk] + xk, ["mn%s_%d" % (s, i)], W)
                mms([(pd, T.W2[:, 15 - i:143 - i], T.mn[:, W * (15 * u + i):W * (15 * u + i + 1)], False, i == nl - 1) for i in range(c, d)],
                    ["W2"] + ["mn%s_%d" % (s, i) for i in range(c, d)], ["pd" + s], W)
        part(0, nl - late, lambda i: T.xg[:, o + i:o + 16 * W:16], ["xg" + s, "xh" + s])
        if late:
            act(un("xl", u), xw(t).indirect(tab("LL", u)), ACT.Identity, 160.0, 1.0, new + ["LL" + s], ["xl" + s] + (["~L"] if j < SOFT else []), W, GAT)
            part(nl - 1, nl, lambda i: un("xl", u), ["xl" + s])

    def choose(t, u, step):
        s = str(u)
        k = "sA%d" % step
        ts(un("ok", u), T["pd" + s][:, 0:W], col("thr%d" % step) if step else 68.0, None, ALU.is_lt, None,
           ["pd" + s] + (["cthr%d" % step] if step else []), ["ok" + s], W)
        mms([(reg(u, 2), T.IDh[:], un("AT", u), True, False), (reg(u, 2), T["TRI%d" % t][:], un("ok", u), False, True)],
            ["IDh", "AT" + s, "TRI%d" % t, "ok" + s], ["pc" + s], W)
        ts(un(k, u), reg(u, 2), -2.0 * LOW, -float(LOW), ALU.add, ALU.max, ["pc" + s], [k + s], W)
        if step < S - 1:
            mms([(reg(u, 3), T.BOh[:], un(k, u), True, True)], ["BOh", k + s], ["pc" + s], W)
            own("sc", u, 3)
            ts(tab("NL", u), last16("sc", u), col("oNL"), None, ALU.add, None, ["sc" + s, "coNL"], ["NL" + s], WB)
        else:
            mms([(reg(u, 3), T.IDh[:], T.MKs[:], True, False), (reg(u, 3), T.BOh[:], un(k, u), False, True),
                 (reg(u, 1), T.BOh[:], un(k, u), True, True)], ["IDh", "MKs", "BOh", k + s], ["pc" + s], W)
            scan(un("sc", u), T.D1[:], reg(u, 3), BIG, ALU.min, ALU.max, ["D1", "pc" + s], ["sc" + s], W)
            ts(tab("NL", u), last16("sc", u), float(CEN + B), None, ALU.add, None, ["sc" + s], ["NL" + s], WB)

    peers = [T.cores[q] for q in range(NR) if q != rank]

    def finish(t, u, j, keys):
        s = str(u)
        act(un("yg", u), xw(t).indirect(tab("NL", u)), ACT.Identity, 160.0, 1.0, keys + ["NL" + s], ["yg" + s], W, GAT)
        if j >= GV:
            tt(un("gt", u), xw(t).indirect(tab("NL", u)), un("zr", u), ALU.is_gt, keys + ["NL" + s, "zr" + s], ["gt" + s], W, 1, GAT)
        else:
            tt(un("gt", u), un("yg", u), un("z", u), ALU.is_gt, ["yg" + s, "z" + s], ["gt" + s], W)
        ts(un("vb", u), reg(u, 1), 15.0 * LOW, None, ALU.add, None, ["pc" + s], ["vb" + s], W)
        mms([(reg(u, 4), T.IDb[:], T.MKv[:], True, False), (reg(u, 4), T.BOn[:], un("gt", u), False, True)],
            ["IDb", "MKv", "BOn", "gt" + s], ["pc" + s], W)
        scan(un("sv", u), T.D2[:], reg(u, 4), BIG, ALU.min, ALU.max, ["D2", "pc" + s], ["sv" + s], W)
        d = (u - rank) % NR
        turn = T.PH[:, 128 - 16 * d:256 - 16 * d]
        mms([(reg(u, 0), turn, un("z", u), True, False), (reg(u, 0), turn, un("yg", u), False, True)], ["PH", "yg" + s, "z" + s], ["pc" + s], W)
        act(un("zt", u), reg(u, 0), ACT.Identity, 1.0, 1.0, ["pc" + s], ["zt" + s], W)
        if t == RO - 1:
            act(un("vout", u), reg(u, 1), ACT.Identity, 15.0 * LOW + CEN, 1.0, ["pc" + s], ["vout" + s], W)
        if d == 0:
            c0 = B + W0N + K * t + W * rank
            act(T.X[:, c0:c0 + W], un("zt", u), ACT.Identity, -160.0, 1.0, ["zt" + s], ["Xo%d" % t], W)
        else:
            k = u if u < rank else u - 1
            act(T.snd[:, W * k:W * k + W], un("zt", u), ACT.Identity, -160.0, 1.0, ["zt" + s], ["snd%d" % k], W)
        act(un("VX", u), un("yg", u), ACT.Identity, col("fb"), col("fs"), ["yg" + s, "cfb", "cfs"], ["VX" + s], W)

    def after(t, u, j):
        s = str(u)
        if j < NLATE:
            prep(t, u)
        else:
            ts(un("AT", u), aw(t).indirect(tab("NL", u)), -float(CEN), None, ALU.add, None, AK + ["NL" + s], ["AT" + s], W, 1, GAT)
        mms([(reg(u, 5), T.IDh[:], un("AT", u), True, False), (reg(u, 5), T.IDh[:], un("NW%d" % t, u), False, True)],
            ["IDh", "AT" + s, "NW%d" % t], ["pc" + s], W)
        act(un("VA", u), reg(u, 5), ACT.Identity, col("va%d" % t), 1.0, ["pc" + s, "cva%d" % t], ["VA" + s], W)
        c0 = B + W0N + K * t + W * u
        ts(T.A[:, c0:c0 + W], un("AT", u), col("m15"), col("nw15"), ALU.mult, ALU.add, ["AT" + s, "cm15", "cnw15"], ["An%d%s" % (t, s)], W)

    def send(t, units, last):
        used = []
        trs = []
        c0 = B + W0N + K * t + W * rank
        ks = [u if u < rank else u - 1 for u in units]
        for k in sorted(ks, key=lambda k: len(topo.engines(core, peers[k]))):
            en = [e for e in topo.engines(core, peers[k]) if e not in used][:ENG]
            used += en
            rid, pid = topo.addr(peers[k])[:2]
            trs.append(RemoteDMATransfer(dst_ids=[DstId(rid=rid, pnc=pid)], dma_engine_mask=sum(1 << e for e in en),
                                         remote_sem=T.sem["arr%d" % t], src=T.snd[:, W * k:W * k + W], dst=T.X[:, c0:c0 + W]))
        rec("G", "send", lambda: g.remote_dma_fused(trs, local_sem=T.sem["snt%d" % last]), ["snd%d" % k for k in ks],
            ["Xa%d" % t if last else "Xb%d" % t], 1.2, 4.0, ("arr%d" % t, "snt%d" % last, ENG * len(ks)))

    ORD = sorted(range(NU), key=lambda u: (u == rank, topo.chip(T.cores[u]) == topo.chip(core), u))
    LAST = NU - 1
    CUT = W * LAST
    PX, PA, PY = ("pd%d" % u for u in ORD[:3])

    def ranges(ps, k, a, b):
        p, out = k // WB, []
        for q in range(a, b):
            lo, hi = W * q, W * q + W
            if ps == PA:
                new = [(16 * k, 16 * k + 16, "MA"), (16 * k + 16, hi, "NB")] if q == p else [(lo, hi, "NB")] if ORD[p] < ORD[q] else []
            elif (q == LAST) != (ps == PY):
                new = []
            elif q != p and LAST in (p, q):
                new = [(lo, hi, "NB" if p == LAST else "FB")]
            else:
                new = [(lo, min(hi, 16 * k + 16), "MT"), (max(lo, 16 * k + 16), hi, "MU")]
            for lo, hi, m in new:
                if lo < hi:
                    if out and out[-1][1:] == (lo, m):
                        lo = out.pop()[0]
                    out.append((lo, hi, m))
        return out

    def joint(t, j):
        jobs = [(k, a, b) for p, a, b in PAIRS.get(j, []) for k in range(WB * p, WB * p + WB)]
        for k, a, b in jobs:
            u = ORD[k // WB]
            plain = (k // WB, a) == (LAST, 0)
            ts(T.EQ[:, K * k + W * a:K * k + W * b], T.vb[:, W * a:W * b], T.sc[:, 16 * k + 15:16 * k + 16],
               1.0 if plain else T.sv[:, 16 * k + 15:16 * k + 16], ALU.is_equal, ALU.min,
               ["vb%d" % v for v in ORD[a:b]] + ["sc%d" % u] + ([] if plain else ["sv%d" % u]), ["EQ%d_%d" % (k, a)], W * (b - a), 0.5)
        if j:
            sums(PX, jobs, {1: (0, 2), 2: (2, 3)}.get(j), j == 1, j == LAST)
        if j == LAST:
            sums(PY, jobs, (LAST, NU), True, True)
            if t < RO - 1:
                sums(PA, [(k, a, b) for i in PAIRS for p, a, b in PAIRS[i] for k in range(WB * p, WB * p + WB)], (0, NU), True, True)

    def span(ps):
        return {PX: (0, CUT), PY: (CUT, K), PA: (0, K)}[ps]

    def sums(ps, jobs, base, first, last):
        c0, c1 = span(ps)
        if first:
            mms([(T[ps][:, c0:c1], T.IDh[:], T.MK0[:, c0:c1], True, False)], ["IDh", "MK0"], [ps, "~" + ps], c1 - c0)
        if base:
            mms([(T[ps][:, W * base[0]:W * base[1]], T.IDh[:], T.vb[:, W * base[0]:W * base[1]], False, False)],
                ["IDh", "~" + ps] + ["vb%d" % v for v in ORD[base[0]:base[1]]], [], W * (base[1] - base[0]))
        jobs = [(k, a, ranges(ps, k, a, b)) for k, a, b in jobs if ranges(ps, k, a, b)]
        for i, (k, a, lst) in enumerate(jobs):
            end = last and i == len(jobs) - 1
            mms([(T[ps][:, lo:hi], T[m][:], T.EQ[:, K * k + lo:K * k + hi], False, end and lo == lst[-1][0]) for lo, hi, m in lst],
                [m for _, _, m in lst] + ["EQ%d_%d" % (k, a), "~" + ps] + (["~X"] if ps == PA and AFTER else []),
                [ps, "~" + ps, "~X"] if end else [], sum(max(64, hi - lo) for lo, hi, _ in lst) / len(lst))

    def places(ps, sc, off):
        c0, c1 = span(ps)
        scan(T[sc][:, c0:c1], T.D0[:, c0:c1], T[ps][:, c0:c1], BIG, ALU.min, ALU.max, ["D0", ps] + (["~S"] if ps == PA else []),
             [sc + ps], c1 - c0)
        ts(T[off][:, c0 // 16:c1 // 16], T[sc][:, c0 + 15:c1:16], CEN + B + 0.25, None, ALU.add, None, [sc + ps], [off + ps], 16)
        return T[off][:, c0 // 16:c1 // 16]

    old = XK
    for t in range(RO):
        if t == 0:
            for j, u in enumerate(ORD):
                stage[0] = 1 + j
                prep(t, u)
        else:
            old, XK = XK, XK + ["Xa%d" % (t - 1), "Xb%d" % (t - 1), "Xo%d" % (t - 1)]
        for st in range(S):
            for j, u in enumerate(ORD):
                stage[0] = 20 * t + 1 + NU * st + j
                bulk(t, u, st, j, old, XK)
                choose(t, u, st)
                if st < S - 1:
                    prep(t, u)
                    advance(t, u, st + 1, XK, j)
                else:
                    finish(t, u, j, XK)
                    if j == NU - 3 and SPLIT:
                        send(t, ORD[:j + 1], 0)
                    if j == NU - 2:
                        send(t, ORD[j:j + 1] if SPLIT else ORD[:j + 1], 1)
                    stage[0] = 20 * t + 16.5
                    joint(t, j)
                    if t < RO - 1:
                        stage[0] = 20 * t + 16.7
                        after(t, u, j)
            if t == RO - 1 and st == 0:
                dma("Y", T.yx[1:128:2, 0:AC - B], T.X[1:128:2, B:AC], "dE", XK, [], 5.0)
        stage[0] = 20 * t + 16.6
        for ps, us in ((PX, ORD[:LAST]), (PY, ORD[LAST:])):
            c0, c1 = span(ps)
            cp(xw(t).indirect(places(ps, "scX", "OFX")), T.VX[:, c0:c1], ["VX%d" % u for u in us] + ["OFX" + ps], XK + ["~S"], c1 - c0, SCA)
        if t < RO - 1:
            stage[0] = 20 * t + 17
            cp(aw(t).indirect(places(PA, "scA", "OFA")), T.VA[:], ["VA%d" % u for u in range(NU)] + ["OFA" + PA], AK, K, SCA)
            AK = AK + ["An%d%d" % (t, u) for u in range(NU)]
    dma("Y", T.yx[0:128:2, 0:AC - B], T.X[0:128:2, B:AC], "dO", XK, [], 4.0)
    dma("Y", T.yx[:, AC - B:XC - B], T.X[:, AC:XC], "dO", ["Xa%d" % (RO - 1), "Xb%d" % (RO - 1), "Xo%d" % (RO - 1)], [], 2.5)
    dma("Y", T.yv[:], T.vout[0:128:16, :], "dO", ["vout%d" % u for u in range(NU)], [], 2.0)

    n = len(recs)
    preds = [{} for _ in range(n)]
    lw, lr = {}, {}

    def bank(k):
        return k[0] == "p"

    for i, r in enumerate(recs):
        reads, writes = r[3], r[4]
        for k in reads + writes:
            for j in ([lw[k]] if k in lw else []) + (lr.get(k, []) if k in writes else []):
                preds[i][j] = preds[i].get(j, False) or not (k[0] in "p~" and recs[j][0] == r[0])
        for k in reads:
            lr.setdefault(k, []).append(i)
        for k in reads + writes:
            if bank(k) or k in writes:
                lw[k] = i
                lr[k] = []
        preds[i].pop(i, None)
    succ = [[] for _ in range(n)]
    for i in range(n):
        for j in preds[i]:
            succ[j].append(i)
    prio = [0.0] * n
    for i in range(n - 1, -1, -1):
        prio[i] = recs[i][5] + recs[i][6] + max([prio[j] + WK * preds[j][i] for j in succ[i]], default=0.0)

    def schedule(before, behind, key, back):
        left = [len(p) for p in before]
        ready = [0.0] * n
        start = [0.0] * n
        avail = {q: [] for q in QUE}
        for i in range(n):
            if left[i] == 0:
                avail[recs[i][0]].append(i)
                ready[i] = recs[i][6] if back else 0.0
        tq = {q: 0.0 for q in QUE}
        order = []
        while len(order) < n:
            e, q = min((min(max(tq[q], ready[i]) for i in avail[q]), q) for q in QUE if avail[q])
            i = max((i for i in avail[q] if max(tq[q], ready[i]) <= e + LOOK[q]), key=key)
            avail[q].remove(i)
            start[i] = max(tq[q], ready[i])
            tq[q] = start[i] + recs[i][5]
            order.append(i)
            for j in behind[i]:
                hard = preds[i][j] if back else preds[j][i]
                ready[j] = max(ready[j], tq[q] + (recs[j if back else i][6] + WK if hard else 0.0))
                left[j] -= 1
                if left[j] == 0:
                    avail[recs[j][0]].append(j)
        return max(start[i] + recs[i][5] + (0 if back else recs[i][6]) for i in range(n)), order, start

    best = cur = schedule(preds, succ, lambda j: (-recs[j][8], prio[j], -j), False)
    for _ in range(TURNS):
        fw = cur[2]
        bw = schedule(succ, preds, lambda j: fw[j] + recs[j][5], True)[2]
        cur = schedule(preds, succ, lambda j: (-min(recs[j][8], 1), -j if recs[j][1] == "dma" else bw[j] + recs[j][5]), False)
        if cur[0] < best[0]:
            best = cur
    order = best[1]

    cnt = {}
    known = {q: {} for q in QUE}
    lastw, lastr = {}, {}

    def need(q, tok):
        sem, val, clk = tok
        kn = known[q]
        if kn.get(sem, 0) >= val:
            return
        QUE[q].wait_ge(T.sem[sem], val)
        kn[sem] = val
        for s_, v_ in clk.items():
            if kn.get(s_, 0) < v_:
                kn[s_] = v_

    total = {}
    for r in recs:
        if r[1] == "dma":
            total[r[7]] = total.get(r[7], 0) + 16
    for i in order:
        q, kind, fn, reads, writes, dur, lat, sem, stg = recs[i]
        reads, writes = [k for k in reads if k[0] != "~"], [k for k in writes if k[0] != "~"]
        toks = []
        for k in reads:
            if bank(k):
                toks += [x for q2, x in lastr.get(k, {}).items() if q2 != q]
            elif k in lastw:
                toks.append(lastw[k])
        for k in writes:
            if k in lastw:
                toks.append(lastw[k])
            toks += [x for q2, x in lastr.get(k, {}).items() if q2 != q or not bank(k)]
        for x in sorted(toks, key=lambda x: -x[1]):
            need(q, x)
        if kind == "op":
            sm = "q" + q
            cnt[sm] = cnt.get(sm, 0) + 1
            fn().then_inc(T.sem[sm], 1)
            tok = rtok = (sm, cnt[sm], dict(known[q]))
            who = q
        elif kind == "dma":
            fn().then_inc(T.sem[sem], 16)
            cnt[sem] = total[sem]
            tok = rtok = (sem, total[sem], dict(known[q]) if total[sem] == 16 else {})
            who = q + sem
        else:
            fn()
            sem, who, m = sem
            cnt[who] = cnt.get(who, 0) + m
            rtok = (who, cnt[who], dict(known[q]))
            cnt[sem] = ENG * len(peers)
            tok = (sem, cnt[sem], {})
        for k in writes:
            if bank(k):
                lastr.setdefault(k, {})[q] = tok
            else:
                lastw[k] = tok
                lastr[k] = {}
        for k in reads:
            lastr.setdefault(k, {})[who] = rtok
    for sem, val in cnt.items():
        need("Y", (sem, val, {}))
